import numpy as np
import ml_dtypes


def mxq(x, axis, fmt="e4m3"):
    dtype, down = {"e4m3": (ml_dtypes.float8_e4m3fn, 7), "e5m2": (ml_dtypes.float8_e5m2, 14)}[fmt]
    v = np.moveaxis(np.asarray(x, np.float32).astype(ml_dtypes.bfloat16).astype(np.float64), axis, -1)
    blocks = v.reshape(v.shape[:-1] + (-1, 32))
    amax = np.abs(blocks).max(-1, keepdims=True)
    byte = np.maximum(np.where(amax > 0, np.frexp(amax)[1] - 1 + 127, 0) - down, 1)
    scale = np.exp2(byte - 127.0)
    codes = (blocks / scale).astype(np.float32).astype(dtype).astype(np.float64)
    return np.moveaxis((codes * scale).reshape(v.shape), -1, axis)


WIDE = False


def mx_kscale(k):
    if not WIDE:
        return np.ones(k)
    levels = np.array([10, -10, 5, -5, 0])
    if k % 512:
        return np.exp2(np.random.permutation(np.resize(levels, k // 32))).repeat(32)
    a = np.empty((k // 512, 16))
    for p in range(k // 512):
        a[p, :8] = np.random.permutation(np.resize(levels, 8))
        for g in range(8):
            far = levels[np.abs(levels - a[p, g]) >= 10]
            a[p, g + 8] = far[np.random.randint(len(far))]
    return np.exp2(a.ravel()).repeat(32)


BF16 = ml_dtypes.bfloat16


def bf(x):
    return np.asarray(x, np.float32).astype(BF16)


def f64(x):
    return np.asarray(x).astype(np.float64)


E2M1 = np.array([0.0, 0.5, 1.0, 1.5, 2.0, 3.0, 4.0, 6.0, -0.0, -0.5, -1.0, -1.5, -2.0, -3.0, -4.0, -6.0])


def pack_weight(w, fmt):
    k, n = w.shape
    w = f64(bf(w)).reshape(k // 32, 32, n)
    amax = np.abs(w).max(1)
    if fmt == "e4m3":
        byte = np.frexp(amax)[1] - 1 + 127 - 7
    else:
        mant, ex = np.frexp(amax / 6.0)
        byte = np.where(mant > 0.5, ex, ex - 1) + 127
    byte = np.clip(np.where(amax > 0, byte, 1), 1, 254)
    scaled = (w * np.exp2(127.0 - byte)[:, None, :]).reshape(k, n).astype(np.float32)
    by_word = np.ascontiguousarray(scaled.reshape(k // 512, 128, 4, n).transpose(0, 1, 3, 2))
    if fmt == "e4m3":
        words = by_word.astype(ml_dtypes.float8_e4m3fn).view(np.uint8)
    else:
        c = by_word.astype(ml_dtypes.float4_e2m1fn).view(np.uint8) & 0xF
        words = c[..., 0::2] | (c[..., 1::2] << 4)
    return np.ascontiguousarray(words), np.ascontiguousarray(byte.astype(np.uint8).reshape(k // 512, 16, n))


def unpack_weight(words, scales, fmt):
    g, p, n, _ = words.shape
    if fmt == "e4m3":
        vals = np.ascontiguousarray(words).view(ml_dtypes.float8_e4m3fn).astype(np.float64)
    else:
        nib = np.empty((g, p, n, 4), np.uint8)
        nib[..., 0::2] = words & 0xF
        nib[..., 1::2] = words >> 4
        vals = E2M1[nib]
    vals = vals * np.repeat(np.exp2(scales.astype(np.float64) - 127.0), 8, axis=1)[..., None]
    return vals.transpose(0, 1, 3, 2).reshape(g * 512, n)


N, I, Z = 1024, 2048, 512


def logsumexp(v):
    m = v.max(axis=-1, keepdims=True)
    return m + np.log(np.sum(np.exp(v - m), axis=-1, keepdims=True))


def gaussian_kl_mean(mu, lv):
    per_dim = 0.5 * (mu * mu + np.exp(lv) - 1.0 - lv)
    return np.mean(per_dim, axis=-1)


def draw0():
    s, t = mx_kscale(I), mx_kscale(Z)
    x = np.random.standard_normal((N, I)) * s
    wm = np.random.standard_normal((I, Z)) / np.sqrt(I) / s[:, None]
    wv = (0.6 * np.random.standard_normal((I, Z)) + 0.4 * np.random.standard_normal((I, 1))) / np.sqrt(I) / s[:, None]
    eps = np.random.standard_normal((N, Z))
    g = (1.0 + 0.2 * np.random.standard_normal(Z)) * t
    wd = 1.5 * np.random.standard_normal((Z, I)) / np.sqrt(Z) / t[:, None]
    bd = 0.5 * np.random.standard_normal(I)
    wm_words, wm_scales = pack_weight(wm, "e4m3")
    wv_words, wv_scales = pack_weight(wv, "e4m3")
    wd_words, wd_scales = pack_weight(wd, "e4m3")
    return {"x": bf(x), "wm_words": wm_words, "wm_scales": wm_scales, "wv_words": wv_words, "wv_scales": wv_scales, "eps": bf(eps), "g": bf(g), "wd_words": wd_words, "wd_scales": wd_scales, "bd": bf(bd)}


def core(x, wm_words, wm_scales, wv_words, wv_scales, eps, g, wd_words, wd_scales, bd):
    xq = mxq(f64(x), 1, "e4m3")
    mu = xq @ unpack_weight(wm_words, wm_scales, "e4m3")
    lv = xq @ unpack_weight(wv_words, wv_scales, "e4m3")
    z = mu + np.exp(0.5 * lv) * f64(eps)
    zg = z * f64(g)[None, :]
    t = (mxq(zg, 1, "e4m3") @ unpack_weight(wd_words, wd_scales, "e4m3")) + f64(bd)[None, :]
    logp = t - logsumexp(t)
    kl = gaussian_kl_mean(mu, lv)
    return logp, kl


def e4m3fn_bytes(y):
    return np.clip(np.asarray(y, np.float64), -448.0, 448.0).astype(np.float32).astype(ml_dtypes.float8_e4m3fn).view(np.uint8)


def e4m3fn_values(b):
    return np.asarray(b, np.uint8).view(ml_dtypes.float8_e4m3fn).astype(np.float64)


def setup_inputs():
    d = draw0()
    x0 = np.asarray(d['x']).astype(np.float64)
    s = (np.max(np.abs(x0), axis=(0,), keepdims=True) / 448.0).astype(np.float32)
    out = {}
    for k, v in d.items():
        if k == 'x':
            out['x_bytes'] = e4m3fn_bytes(x0 / s.astype(np.float64))
            out['x_scale'] = s
        else:
            out[k] = v
    return out


def reference(x_bytes, x_scale, wm_words, wm_scales, wv_words, wv_scales, eps, g, wd_words, wd_scales, bd):
    return core(e4m3fn_values(x_bytes) * x_scale.astype(np.float64), wm_words, wm_scales, wv_words, wv_scales, eps, g, wd_words, wd_scales, bd)

@@ -1,0 +1,410 @@
+import math
+from contextlib import ExitStack
+
+import concourse.mybir as mybir
+from concourse.masks import make_identity
+
+N, I, Z = 1024, 2048, 512
+FLOPS = 3 * 2 * N * I * Z
+
+F32 = mybir.dt.float32
+BF16 = mybir.dt.bfloat16
+I32 = mybir.dt.int32
+U32 = mybir.dt.uint32
+U8 = mybir.dt.uint8
+FP8 = mybir.dt.float8_e4m3fn
+FP8X4 = mybir.dt.float8_e4m3fn_x4
+ALU = mybir.AluOpType
+ACT = mybir.ActivationFunctionType
+AXIS = mybir.AxisListType
+
+P = 128
+TILES = N // P
+PASSES = I // 512
+BANK = 512
+CHUNKS = I // BANK
+HALF = I // 2
+LN2 = math.log(2.0)
+
+
+def tile_linearvaeitemlogsoftmax_w8_kernel(
+    tc, x_bytes, x_scale, wm_words, wm_scales, wv_words, wv_scales, eps, g, wd_words, wd_scales, bd, out_0, out_1
+):
+    nc = tc.nc
+    x_rows = x_bytes.rearrange("(p i) k -> p i k", i=TILES)
+    eps_rows = eps.rearrange("(p i) z -> p i z", i=TILES)
+    logp_rows = out_0.rearrange("(p i) n -> p i n", i=TILES)
+
+    with ExitStack() as ctx:
+        keep = ctx.enter_context(tc.tile_pool(name="keep", bufs=1))
+        work = ctx.enter_context(tc.tile_pool(name="work", bufs=2))
+        psum = ctx.enter_context(tc.psum_pool(name="psum", bufs=1))
+        ctx.enter_context(tc.manual_schedule())
+
+        w_scales = keep.tile([P, 3, BANK], U8, align_bytes=64)
+        nc.vector.memset(w_scales[:].rearrange("p w n -> p (w n)").bitcast(I32), 0)
+        ident = keep.tile([P, P], F32)
+        make_identity(nc, ident[:])
+        consts = keep.tile([P, 3], F32)
+        for col, value in enumerate((-1.5, -1.0, -2.0)):
+            nc.gpsimd.memset(consts[:, col : col + 1], value)
+        minus_3_halves, minus_one, minus_two = (consts[:, col : col + 1] for col in range(3))
+
+        x_sb = [keep.tile([P, I], U8, name="x_codes_%d" % i) for i in range(TILES)]
+        x_scale_sb = keep.tile([P, PASSES, 4], F32)
+        wm_sb = keep.tile([P, PASSES, Z], U32, align_bytes=64)
+        wv_sb = keep.tile([P, PASSES, Z], U32, align_bytes=64)
+        wd_sb = keep.tile([P, I], U32, align_bytes=64)
+        eps_sb = [keep.tile([P, TILES // 2, Z], BF16, name="eps_%d" % h) for h in range(2)]
+        g_sb = keep.tile([P, 4], BF16)
+        bd_sb = keep.tile([P, I], BF16)
+
+        def load_x(i):
+            nc.sync.dma_start(out=x_sb[i][:], in_=x_rows[:, i, :])
+
+        def load_scales(slot, rows):
+            for q in range(4):
+                nc.sync.dma_start(
+                    out=w_scales[32 * q : 32 * q + 16, slot, :].bitcast(I32),
+                    in_=rows[:, 4 * q : 4 * q + 4, :].bitcast(I32),
+                )
+
+        def load_words(dst, words):
+            src = words.rearrange("g p n t -> p g (n t)").bitcast(I32)
+            nc.sync.dma_start(out=dst[:].bitcast(I32), in_=src)
+
+        def load_eps(h):
+            nc.sync.dma_start(out=eps_sb[h][:], in_=eps_rows[:, 4 * h : 4 * h + 4, :])
+
+        load_x(0)
+        nc.sync.dma_start(out=x_scale_sb[:], in_=x_scale.rearrange("o (g p t) -> p (o g) t", p=P, t=4))
+        load_x(1)
+        load_scales(1, wv_scales)
+        load_words(wv_sb, wv_words)
+        load_x(2)
+        load_scales(0, wm_scales)
+        load_words(wm_sb, wm_words)
+        load_eps(0)
+        load_x(3)
+        nc.sync.dma_start(out=g_sb[:], in_=g.rearrange("(p t) -> p t", t=4))
+        load_scales(2, wd_scales[0].rearrange("r (c n) -> c r n", n=BANK))
+        nc.sync.dma_start(out=wd_sb[:].bitcast(I32), in_=wd_words[0].rearrange("p n t -> p (n t)").bitcast(I32))
+        load_x(4)
+        nc.sync.dma_start(out=bd_sb[:], in_=bd.partition_broadcast(P))
+        load_x(5)
+        load_eps(1)
+        load_x(6)
+        load_x(7)
+
+        neg_max = keep.tile([P, TILES], F32)
+        neg_lse = keep.tile([P, TILES], F32)
+        exp_sum = keep.tile([P, TILES], F32)
+        lv_sum = keep.tile([P, TILES], F32)
+        sq_sum = keep.tile([P, 2, TILES], F32)
+        log_steps = keep.tile([P, 8, TILES], F32)
+
+        wide, x_bank, x_grouped, x_mx, lv_bank, mu_bank, mu_sd, noise = {}, {}, {}, {}, {}, {}, {}, {}
+        z_bank, z_grouped, z_mx, t_bank, logits = {}, {}, {}, {}, {}
+
+        def widen(i, h):
+            wide[i, h] = work.tile([P, HALF], BF16, name="wide", bufs=5)
+            nc.scalar.copy(out=wide[i, h][:], in_=x_sb[i][:, h * HALF : (h + 1) * HALF].bitcast(FP8))
+
+        def turn_x(i, h):
+            x_bank[i, h] = psum.tile([P, 2, 2, P], F32, name="x_bank", bufs=2)
+            words = wide[i, h][:].bitcast(F32)
+            for gl in range(2):
+                for u in range(2):
+                    nc.tensor.transpose(x_bank[i, h][:, u, gl, :], words[:, 256 * gl + u : 256 * (gl + 1) : 2], ident[:])
+
+        def scale_x(i, h):
+            if h == 0:
+                x_grouped[i] = work.tile([P, PASSES, P, 4], BF16, name="x_grouped", bufs=3, align_bytes=64)
+            nc.vector.tensor_tensor(
+                out=x_grouped[i][:, 2 * h : 2 * h + 2].rearrange("p g k (u e) -> p g k u e", u=2),
+                in0=x_bank[i, h][:].bitcast(BF16).rearrange("p u g (k e) -> p g k u e", e=2),
+                in1=x_scale_sb[:, 2 * h : 2 * h + 2, :]
+                .rearrange("p g (u e) -> p g u e", u=2)
+                .unsqueeze(2)
+                .broadcast_to([P, 2, P, 2, 2]),
+                op=ALU.mult,
+            )
+
+        def quantize(name, grouped, words):
+            codes = work.tile([P, words], U32, name=name + "_codes", bufs=4, align_bytes=64)
+            scales = work.tile([P, words], U8, name=name + "_scales", bufs=4, align_bytes=64)
+            nc.vector.quantize_mx(out=codes[:].bitcast(FP8X4), scales=scales[:], in_=grouped)
+            return codes, scales
+
+        def quantize_x(i):
+            x_mx[i] = quantize("xq", x_grouped[i][:].rearrange("p g k t -> p (g k t)"), PASSES * P)
+
+        def encode(i, bank, w_sb, slot, passes):
+            codes, scales = x_mx[i]
+            for k in passes:
+                cols = slice(k * P, (k + 1) * P)
+                nc.tensor.matmul_mx(
+                    out=bank[:],
+                    lhsT=codes[:, cols].bitcast(FP8X4),
+                    lhsT_scale=scales[:, cols],
+                    rhs=w_sb[:, k, :].bitcast(FP8X4),
+                    rhs_scale=w_scales[4 * k :, slot, :],
+                    start=(k == 0),
+                    stop=(k == PASSES - 1),
+                )
+
+        def encode_lv(i):
+            lv_bank[i] = psum.tile([P, Z], F32, name="lv_bank")
+            encode(i, lv_bank[i], wv_sb, 1, range(PASSES))
+
+        def encode_mu(i):
+            mu_bank[i] = psum.tile([P, Z], F32, name="mu_bank")
+            encode(i, mu_bank[i], wm_sb, 0, range(PASSES))
+
+        def by_slot(ap):
+            return ap.rearrange("p (m t) -> p t m", t=4)
+
+        def unread(width):
+            scratch = work.tile([P, I], BF16, name="unread")
+            return scratch[:, :width]
+
+        def deviation(i):
+            mu_sd[i] = work.tile([P, 2, 4, P], F32, name="mu_sd", bufs=3)
+            nc.scalar.activation(out=mu_sd[i][:, 1], in_=by_slot(lv_bank[i][:]), func=ACT.Exp, scale=0.5)
+
+        def sum_lv(i):
+            nc.scalar.activation(out=unread(Z), in_=lv_bank[i][:], func=ACT.Identity, accum_out=lv_sum[:, i : i + 1])
+
+        def copy_mu(i):
+            nc.scalar.copy(out=mu_sd[i][:, 0], in_=by_slot(mu_bank[i][:]))
+
+        def sum_squares(i, a):
+            nc.scalar.activation(
+                out=unread(Z),
+                in_=mu_sd[i][:, a].rearrange("p t m -> p (t m)"),
+                func=ACT.Square,
+                accum_out=sq_sum[:, a, i : i + 1],
+            )
+
+        def sample(i):
+            noise[i] = work.tile([P, 4, P], F32, name="noise", bufs=3)
+            nc.gpsimd.tensor_tensor(
+                out=noise[i][:], in0=mu_sd[i][:, 1], in1=by_slot(eps_sb[i // 4][:, i % 4, :]), op=ALU.mult
+            )
+
+        def turn_z(i):
+            z_bank[i] = psum.tile([P, 4, P], F32, name="z_bank")
+            for t in range(4):
+                for first, term in ((True, mu_sd[i][:, 0, t, :]), (False, noise[i][:, t, :])):
+                    nc.tensor.matmul(
+                        out=z_bank[i][:, t, :], lhsT=term, rhs=ident[:], is_transpose=True, start=first, stop=not first
+                    )
+
+        def gain_z(i):
+            z_grouped[i] = work.tile([P, P, 4], BF16, name="z_grouped", align_bytes=64)
+            nc.vector.tensor_tensor(
+                out=z_grouped[i][:],
+                in0=z_bank[i][:].rearrange("p t k -> p k t"),
+                in1=g_sb[:].unsqueeze(1).broadcast_to([P, P, 4]),
+                op=ALU.mult,
+            )
+
+        def quantize_z(i):
+            z_mx[i] = quantize("zq", z_grouped[i][:].rearrange("p k t -> p (k t)"), P)
+
+        def decode(i, c):
+            t_bank[i, c] = psum.tile([P, BANK], F32, name="t_bank", bufs=3)
+            codes, scales = z_mx[i]
+            nc.tensor.matmul_mx(
+                out=t_bank[i, c][:],
+                lhsT=codes[:].bitcast(FP8X4),
+                lhsT_scale=scales[:],
+                rhs=wd_sb[:, c * BANK : (c + 1) * BANK].bitcast(FP8X4),
+                rhs_scale=w_scales[4 * c :, 2, :],
+                start=True,
+                stop=True,
+            )
+
+        def add_bias(i, c):
+            if c == 0:
+                logits[i] = work.tile([P, I], F32, name="logits", bufs=5)
+            cols = slice(c * BANK, (c + 1) * BANK)
+            nc.vector.tensor_tensor(out=logits[i][:, cols], in0=t_bank[i, c][:], in1=bd_sb[:, cols], op=ALU.add)
+
+        def row_max(i):
+            nc.vector.tensor_reduce(out=neg_max[:, i : i + 1], in_=logits[i][:], axis=AXIS.X, op=ALU.max, negate=True)
+
+        def sum_exp(i):
+            nc.scalar.activation(
+                out=unread(I),
+                in_=logits[i][:],
+                func=ACT.Exp,
+                bias=neg_max[:, i : i + 1],
+                accum_out=exp_sum[:, i : i + 1],
+            )
+
+        def log_step(i, step):
+            total = exp_sum[:, i : i + 1]
+            u0, e0, q, u1, e1, u2, e2, y = (log_steps[:, row, i : i + 1] for row in range(8))
+            if step == 0:
+                nc.scalar.activation(
+                    out=u0, in_=total.bitcast(U32), func=ACT.Copy, scale=LN2 / 2**23, bias=(0.043 - 127.0) * LN2 - 1.5
+                )
+            elif step == 1:
+                nc.scalar.activation(out=e0, in_=u0, func=ACT.Exp, scale=-1.0, bias=minus_3_halves)
+            elif step == 2:
+                nc.scalar.activation(out=q, in_=e0, func=ACT.Square, scale=total, bias=minus_two)
+            elif step == 3:
+                nc.scalar.activation(out=u1, in_=q, func=ACT.Identity, scale=-0.5, bias=u0)
+            elif step == 4:
+                nc.scalar.activation(out=e1, in_=u1, func=ACT.Exp, scale=-1.0, bias=minus_two)
+            elif step == 5:
+                nc.scalar.activation(out=u2, in_=e1, func=ACT.Identity, scale=total, bias=u1)
+            elif step == 6:
+                nc.scalar.activation(out=e2, in_=u2, func=ACT.Exp, scale=-1.0, bias=minus_one)
+            else:
+                nc.scalar.activation(out=y, in_=e2, func=ACT.Identity, scale=total, bias=u2)
+
+        def finish(i):
+            col = slice(i, i + 1)
+            nc.vector.tensor_tensor(out=neg_lse[:, col], in0=neg_max[:, col], in1=log_steps[:, 7, col], op=ALU.subtract)
+            nc.gpsimd.tensor_scalar(
+                out=logits[i][:], in0=logits[i][:], scalar1=1.0, scalar2=neg_lse[:, col], op0=ALU.mult, op1=ALU.add
+            )
+            nc.sync.dma_start(out=logp_rows[:, i, :], in_=logits[i][:])
+
+        def finish_on_vector(i):
+            col = slice(i, i + 1)
+            for h in range(2):
+                cols = slice(h * HALF, (h + 1) * HALF)
+                nc.vector.tensor_scalar(
+                    out=logits[i][:, cols], in0=logits[i][:, cols], scalar1=neg_max[:, col], scalar2=log_steps[:, 7, col],
+                    op0=ALU.add, op1=ALU.subtract,
+                )
+                nc.sync.dma_start(out=logp_rows[:, i, cols], in_=logits[i][:, cols])
+
+        def finish_kl():
+            kl = keep.tile([P, TILES], F32)
+            nc.gpsimd.tensor_tensor(out=kl[:], in0=sq_sum[:, 1], in1=lv_sum[:], op=ALU.subtract)
+            nc.gpsimd.tensor_tensor(out=kl[:], in0=kl[:], in1=sq_sum[:, 0], op=ALU.add)
+            nc.gpsimd.tensor_scalar(out=kl[:], in0=kl[:], scalar1=0.5 / Z, scalar2=-0.5, op0=ALU.mult, op1=ALU.add)
+            nc.sync.dma_start(out=out_1.rearrange("(p i) -> p i", i=TILES), in_=kl[:])
+
+        part = keep.tile([P, CHUNKS], F32)
+        part_sum = keep.tile([P, 2, CHUNKS], F32)
+        tail = keep.tile([P, 2, CHUNKS], F32)
+        log_total = keep.tile([P, 1], F32)
+
+        def chunk_max(i, c):
+            nc.vector.tensor_reduce(
+                out=part[:, c : c + 1], in_=logits[i][:, c * BANK : (c + 1) * BANK], axis=AXIS.X, op=ALU.max, negate=True
+            )
+
+        def chunk_exp(i, c):
+            nc.scalar.activation(
+                out=unread(BANK),
+                in_=logits[i][:, c * BANK : (c + 1) * BANK],
+                func=ACT.Exp,
+                bias=part[:, c : c + 1],
+                accum_out=part_sum[:, 0, c : c + 1],
+            )
+
+        def join_max(i):
+            nc.vector.tensor_reduce(out=neg_max[:, i : i + 1], in_=part[:], axis=AXIS.X, op=ALU.min)
+
+        def finish_last(i):
+            col = slice(i, i + 1)
+            nc.scalar.activation(out=part_sum[:, 1, :], in_=part[:], func=ACT.Exp, scale=-1.0, bias=neg_max[:, col])
+            nc.vector.scalar_tensor_tensor(
+                out=tail[:, 0, :], in0=part_sum[:, 0, :], scalar=1.0, in1=part_sum[:, 1, :],
+                op0=ALU.mult, op1=ALU.mult, accum_out=tail[:, 1, 0:1],
+            )
+            nc.scalar.activation(out=log_total[:], in_=tail[:, 1, 0:1], func=ACT.Ln)
+            for c in range(CHUNKS):
+                cols = slice(c * BANK, (c + 1) * BANK)
+                nc.vector.tensor_scalar(
+                    out=logits[i][:, cols], in0=logits[i][:, cols], scalar1=neg_max[:, col], scalar2=log_total[:],
+                    op0=ALU.add, op1=ALU.subtract,
+                )
+                nc.sync.dma_start(out=logp_rows[:, i, cols], in_=logits[i][:, cols])
+
+        def run(stage, i, *args, end=TILES):
+            if 0 <= i < end:
+                stage(i, *args)
+
+        LAST = TILES - 1
+        for s in range(-3, LAST + 2):
+            j = s - 2
+            filling = j < 0
+            run(quantize_x, s)
+            run(finish, j - 2)
+            if s == TILES:
+                finish_kl()
+            if filling:
+                run(turn_z, j + 1)
+            run(encode_lv, s)
+            run(sum_exp, j - 1)
+            run(log_step, j - 1, 0)
+            run(scale_x, s + 1, 0)
+            run(add_bias, j, 0)
+            run(decode, j, 3)
+            if not filling:
+                run(turn_z, j + 1)
+            run(deviation, s)
+            run(log_step, j - 1, 1)
+            run(sample, s)
+            run(sum_lv, s)
+            run(log_step, j - 1, 2)
+            run(turn_x, s + 2, 0)
+            for c in range(1, CHUNKS):
+                run(add_bias, j, c)
+            if filling:
+                run(scale_x, s + 1, 1)
+                run(gain_z, j + 1)
+                run(quantize_z, j + 1)
+                for c in range(CHUNKS - 1):
+                    run(decode, j + 1, c)
+                run(encode_mu, s)
+                run(copy_mu, s)
+                run(turn_x, s + 2, 1)
+                run(widen, s + 3, 0)
+                run(widen, s + 3, 1)
+                run(sum_squares, s, 1)
+                run(sum_squares, s, 0)
+            else:
+                run(encode_mu, s)
+                run(gain_z, j + 1)
+                run(scale_x, s + 1, 1)
+                run(quantize_z, j + 1)
+                run(row_max, j)
+                run(turn_x, s + 2, 1)
+                for c in range(CHUNKS - 1):
+                    run(decode, j + 1, c)
+                run(widen, s + 3, 0)
+                run(log_step, j - 1, 3)
+                run(sum_squares, s, 1)
+                run(log_step, j - 1, 4)
+                run(copy_mu, s)
+                run(log_step, j - 1, 5)
+                run(widen, s + 3, 1)
+                run(log_step, j - 1, 6)
+                run(sum_squares, s, 0)
+                run(log_step, j - 1, 7)
+        finish(LAST - 2)
+        sum_exp(LAST - 1)
+        add_bias(LAST, 0)
+        decode(LAST, 3)
+        add_bias(LAST, 1)
+        chunk_max(LAST, 0)
+        add_bias(LAST, 2)
+        chunk_max(LAST, 1)
+        add_bias(LAST, 3)
+        chunk_max(LAST, 2)
+        chunk_max(LAST, 3)
+        join_max(LAST)
+        for c in range(CHUNKS):
+            for step in ((), (0, 1, 2), (3, 4, 5), (6, 7))[c]:
+                log_step(LAST - 1, step)
+            chunk_exp(LAST, c)
+        finish_on_vector(LAST - 1)
+        finish_last(LAST)

@@ -24,6 +24,7 @@ PASSES = I // 512
 BANK = 512
 CHUNKS = I // BANK
 HALF = I // 2
+PSUM_BUFS = {"x_bank": 2, "t_bank": 3, "z_bank": 1}
 LN2 = math.log(2.0)
 
 
@@ -41,6 +42,10 @@ def tile_linearvaeitemlogsoftmax_w8_kernel(
         psum = ctx.enter_context(tc.psum_pool(name="psum", bufs=1))
         ctx.enter_context(tc.manual_schedule())
 
+        bd_row = keep.tile([P, I], BF16)
+        nc.vector.memset(bd_row[:].bitcast(I32), 0)
+        ones = keep.tile([P, P], BF16)
+        nc.vector.memset(ones[:], 1.0)
         w_scales = keep.tile([P, 3, BANK], U8, align_bytes=64)
         nc.vector.memset(w_scales[:].rearrange("p w n -> p (w n)").bitcast(I32), 0)
         ident = keep.tile([P, P], F32)
@@ -55,7 +60,7 @@ def tile_linearvaeitemlogsoftmax_w8_kernel(
         wm_sb = keep.tile([P, PASSES, Z], U32, align_bytes=64)
         wv_sb = keep.tile([P, PASSES, Z], U32, align_bytes=64)
         wd_sb = keep.tile([P, I], U32, align_bytes=64)
-        eps_sb = [keep.tile([P, TILES // 2, Z], BF16, name="eps_%d" % h) for h in range(2)]
+        eps_sb = [keep.tile([P, 2, Z], BF16, name="eps_%d" % h) for h in range(TILES // 2)]
         g_sb = keep.tile([P, 4], BF16)
         bd_sb = keep.tile([P, I], BF16)
 
@@ -73,28 +78,28 @@ def tile_linearvaeitemlogsoftmax_w8_kernel(
             src = words.rearrange("g p n t -> p g (n t)").bitcast(I32)
             nc.sync.dma_start(out=dst[:].bitcast(I32), in_=src)
 
-        def load_eps(h):
-            nc.sync.dma_start(out=eps_sb[h][:], in_=eps_rows[:, 4 * h : 4 * h + 4, :])
+        def load_eps(i):
+            nc.sync.dma_start(out=eps_sb[i // 2][:], in_=eps_rows[:, i : i + 2, :])
 
         load_x(0)
+        nc.sync.dma_start(out=bd_row[0:1, :], in_=bd.rearrange("(o n) -> o n", o=1))
         nc.sync.dma_start(out=x_scale_sb[:], in_=x_scale.rearrange("o (g p t) -> p (o g) t", p=P, t=4))
         load_x(1)
-        load_scales(1, wv_scales)
         load_words(wv_sb, wv_words)
+        load_scales(1, wv_scales)
         load_x(2)
-        load_scales(0, wm_scales)
         load_words(wm_sb, wm_words)
         load_eps(0)
+        load_scales(0, wm_scales)
         load_x(3)
+        nc.sync.dma_start(out=wd_sb[:].bitcast(I32), in_=wd_words[0].rearrange("p n t -> p (n t)").bitcast(I32))
         nc.sync.dma_start(out=g_sb[:], in_=g.rearrange("(p t) -> p t", t=4))
         load_scales(2, wd_scales[0].rearrange("r (c n) -> c r n", n=BANK))
-        nc.sync.dma_start(out=wd_sb[:].bitcast(I32), in_=wd_words[0].rearrange("p n t -> p (n t)").bitcast(I32))
-        load_x(4)
-        nc.sync.dma_start(out=bd_sb[:], in_=bd.partition_broadcast(P))
-        load_x(5)
-        load_eps(1)
-        load_x(6)
-        load_x(7)
+        for i in range(4, TILES):
+            load_x(i)
+            if i % 2 == 0:
+                load_eps(i - 2)
+        load_eps(TILES - 2)
 
         neg_max = keep.tile([P, TILES], F32)
         neg_lse = keep.tile([P, TILES], F32)
@@ -106,38 +111,59 @@ def tile_linearvaeitemlogsoftmax_w8_kernel(
         wide, x_bank, x_grouped, x_mx, lv_bank, mu_bank, mu_sd, noise = {}, {}, {}, {}, {}, {}, {}, {}
         z_bank, z_grouped, z_mx, t_bank, logits = {}, {}, {}, {}, {}
 
-        def widen(i, h):
-            wide[i, h] = work.tile([P, HALF], BF16, name="wide", bufs=5)
-            nc.scalar.copy(out=wide[i, h][:], in_=x_sb[i][:, h * HALF : (h + 1) * HALF].bitcast(FP8))
+        bias_bank = {}
 
-        def turn_x(i, h):
-            x_bank[i, h] = psum.tile([P, 2, 2, P], F32, name="x_bank", bufs=2)
-            words = wide[i, h][:].bitcast(F32)
-            for gl in range(2):
+        def spread_bias(h, bank):
+            bias_bank[h] = psum.tile([P, HALF], BF16, name=bank)
+            for c in range(2):
+                src = slice(h * HALF + c * BANK, h * HALF + (c + 1) * BANK)
+                nc.tensor.matmul(
+                    out=bias_bank[h][:, c * BANK : (c + 1) * BANK], lhsT=ones[:], rhs=bd_row[:, src], start=True, stop=True
+                )
+
+        def keep_bias(h):
+            nc.scalar.copy(out=bd_sb[:, h * HALF : (h + 1) * HALF], in_=bias_bank[h][:])
+
+        def widen(i, first, count=2, copy=nc.scalar.copy):
+            wide[i, first] = work.tile([P, count * BANK], BF16, name="wide", bufs=8)
+            copy(out=wide[i, first][:], in_=x_sb[i][:, first * BANK : (first + count) * BANK].bitcast(FP8))
+
+        def turn_x(i, first, count=2, bank="x_bank"):
+            x_bank[i, first] = psum.tile([P, 2, count, P], F32, name=bank, bufs=PSUM_BUFS[bank])
+            words = wide[i, first][:].bitcast(F32)
+            for k in range(count):
                 for u in range(2):
-                    nc.tensor.transpose(x_bank[i, h][:, u, gl, :], words[:, 256 * gl + u : 256 * (gl + 1) : 2], ident[:])
+                    nc.tensor.transpose(x_bank[i, first][:, u, k, :], words[:, 256 * k + u : 256 * (k + 1) : 2], ident[:])
 
-        def scale_x(i, h):
-            if h == 0:
-                x_grouped[i] = work.tile([P, PASSES, P, 4], BF16, name="x_grouped", bufs=3, align_bytes=64)
+        def scale_x(i, first, count=2):
+            if first == 0:
+                x_grouped[i] = work.tile([P, PASSES, P, 4], BF16, name="x_grouped", align_bytes=64)
+            passes = slice(first, first + count)
             nc.vector.tensor_tensor(
-                out=x_grouped[i][:, 2 * h : 2 * h + 2].rearrange("p g k (u e) -> p g k u e", u=2),
-                in0=x_bank[i, h][:].bitcast(BF16).rearrange("p u g (k e) -> p g k u e", e=2),
-                in1=x_scale_sb[:, 2 * h : 2 * h + 2, :]
+                out=x_grouped[i][:, passes].rearrange("p g k (u e) -> p g k u e", u=2),
+                in0=x_bank[i, first][:].bitcast(BF16).rearrange("p u g (k e) -> p g k u e", e=2),
+                in1=x_scale_sb[:, passes, :]
                 .rearrange("p g (u e) -> p g u e", u=2)
                 .unsqueeze(2)
-                .broadcast_to([P, 2, P, 2, 2]),
+                .broadcast_to([P, count, P, 2, 2]),
                 op=ALU.mult,
             )
 
-        def quantize(name, grouped, words):
-            codes = work.tile([P, words], U32, name=name + "_codes", bufs=4, align_bytes=64)
-            scales = work.tile([P, words], U8, name=name + "_scales", bufs=4, align_bytes=64)
-            nc.vector.quantize_mx(out=codes[:].bitcast(FP8X4), scales=scales[:], in_=grouped)
+        def mx_tiles(name, words):
+            codes = work.tile([P, words], U32, name=name + "_codes", align_bytes=64)
+            scales = work.tile([P, words], U8, name=name + "_scales", align_bytes=64)
             return codes, scales
 
-        def quantize_x(i):
-            x_mx[i] = quantize("xq", x_grouped[i][:].rearrange("p g k t -> p (g k t)"), PASSES * P)
+        def quantize_x(i, first=0, count=PASSES):
+            if first == 0:
+                x_mx[i] = mx_tiles("xq", PASSES * P)
+            codes, scales = x_mx[i]
+            cols = slice(first * P, (first + count) * P)
+            nc.vector.quantize_mx(
+                out=codes[:, cols].bitcast(FP8X4),
+                scales=scales[:, cols],
+                in_=x_grouped[i][:, first : first + count].rearrange("p g k t -> p (g k t)"),
+            )
 
         def encode(i, bank, w_sb, slot, passes):
             codes, scales = x_mx[i]
@@ -153,13 +179,15 @@ def tile_linearvaeitemlogsoftmax_w8_kernel(
                     stop=(k == PASSES - 1),
                 )
 
-        def encode_lv(i):
-            lv_bank[i] = psum.tile([P, Z], F32, name="lv_bank")
-            encode(i, lv_bank[i], wv_sb, 1, range(PASSES))
+        def encode_lv(i, first=0, count=PASSES):
+            if first == 0:
+                lv_bank[i] = psum.tile([P, Z], F32, name="lv_bank")
+            encode(i, lv_bank[i], wv_sb, 1, range(first, first + count))
 
-        def encode_mu(i):
-            mu_bank[i] = psum.tile([P, Z], F32, name="mu_bank")
-            encode(i, mu_bank[i], wm_sb, 0, range(PASSES))
+        def encode_mu(i, first=0, count=PASSES):
+            if first == 0:
+                mu_bank[i] = psum.tile([P, Z], F32, name="mu_bank")
+            encode(i, mu_bank[i], wm_sb, 0, range(first, first + count))
 
         def by_slot(ap):
             return ap.rearrange("p (m t) -> p t m", t=4)
@@ -169,7 +197,7 @@ def tile_linearvaeitemlogsoftmax_w8_kernel(
             return scratch[:, :width]
 
         def deviation(i):
-            mu_sd[i] = work.tile([P, 2, 4, P], F32, name="mu_sd", bufs=3)
+            mu_sd[i] = work.tile([P, 2, 4, P], F32, name="mu_sd", bufs=4)
             nc.scalar.activation(out=mu_sd[i][:, 1], in_=by_slot(lv_bank[i][:]), func=ACT.Exp, scale=0.5)
 
         def sum_lv(i):
@@ -189,7 +217,7 @@ def tile_linearvaeitemlogsoftmax_w8_kernel(
         def sample(i):
             noise[i] = work.tile([P, 4, P], F32, name="noise", bufs=3)
             nc.gpsimd.tensor_tensor(
-                out=noise[i][:], in0=mu_sd[i][:, 1], in1=by_slot(eps_sb[i // 4][:, i % 4, :]), op=ALU.mult
+                out=noise[i][:], in0=mu_sd[i][:, 1], in1=by_slot(eps_sb[i // 2][:, i % 2, :]), op=ALU.mult
             )
 
         def turn_z(i):
@@ -210,7 +238,11 @@ def tile_linearvaeitemlogsoftmax_w8_kernel(
             )
 
         def quantize_z(i):
-            z_mx[i] = quantize("zq", z_grouped[i][:].rearrange("p k t -> p (k t)"), P)
+            z_mx[i] = mx_tiles("zq", P)
+            codes, scales = z_mx[i]
+            nc.vector.quantize_mx(
+                out=codes[:].bitcast(FP8X4), scales=scales[:], in_=z_grouped[i][:].rearrange("p k t -> p (k t)")
+            )
 
         def decode(i, c):
             t_bank[i, c] = psum.tile([P, BANK], F32, name="t_bank", bufs=3)
@@ -278,8 +310,12 @@ def tile_linearvaeitemlogsoftmax_w8_kernel(
             for h in range(2):
                 cols = slice(h * HALF, (h + 1) * HALF)
                 nc.vector.tensor_scalar(
-                    out=logits[i][:, cols], in0=logits[i][:, cols], scalar1=neg_max[:, col], scalar2=log_steps[:, 7, col],
-                    op0=ALU.add, op1=ALU.subtract,
+                    out=logits[i][:, cols],
+                    in0=logits[i][:, cols],
+                    scalar1=neg_max[:, col],
+                    scalar2=log_steps[:, 7, col],
+                    op0=ALU.add,
+                    op1=ALU.subtract,
                 )
                 nc.sync.dma_start(out=logp_rows[:, i, cols], in_=logits[i][:, cols])
 
@@ -290,14 +326,18 @@ def tile_linearvaeitemlogsoftmax_w8_kernel(
             nc.gpsimd.tensor_scalar(out=kl[:], in0=kl[:], scalar1=0.5 / Z, scalar2=-0.5, op0=ALU.mult, op1=ALU.add)
             nc.sync.dma_start(out=out_1.rearrange("(p i) -> p i", i=TILES), in_=kl[:])
 
-        part = keep.tile([P, CHUNKS], F32)
-        part_sum = keep.tile([P, 2, CHUNKS], F32)
-        tail = keep.tile([P, 2, CHUNKS], F32)
+        part_max = keep.tile([P, 2, CHUNKS], F32)
+        part_sum = keep.tile([P, 2, 2, CHUNKS], F32)
+        part_term = keep.tile([P, 2, CHUNKS], F32)
         log_total = keep.tile([P, 1], F32)
 
         def chunk_max(i, c):
             nc.vector.tensor_reduce(
-                out=part[:, c : c + 1], in_=logits[i][:, c * BANK : (c + 1) * BANK], axis=AXIS.X, op=ALU.max, negate=True
+                out=part_max[:, i % 2, c : c + 1],
+                in_=logits[i][:, c * BANK : (c + 1) * BANK],
+                axis=AXIS.X,
+                op=ALU.max,
+                negate=True,
             )
 
         def chunk_exp(i, c):
@@ -305,26 +345,41 @@ def tile_linearvaeitemlogsoftmax_w8_kernel(
                 out=unread(BANK),
                 in_=logits[i][:, c * BANK : (c + 1) * BANK],
                 func=ACT.Exp,
-                bias=part[:, c : c + 1],
-                accum_out=part_sum[:, 0, c : c + 1],
+                bias=part_max[:, i % 2, c : c + 1],
+                accum_out=part_sum[:, i % 2, 0, c : c + 1],
             )
 
         def join_max(i):
-            nc.vector.tensor_reduce(out=neg_max[:, i : i + 1], in_=part[:], axis=AXIS.X, op=ALU.min)
+            nc.vector.tensor_reduce(out=neg_max[:, i : i + 1], in_=part_max[:, i % 2], axis=AXIS.X, op=ALU.min)
+
+        def chunk_weights(i):
+            nc.scalar.activation(
+                out=part_sum[:, i % 2, 1], in_=part_max[:, i % 2], func=ACT.Exp, scale=-1.0, bias=neg_max[:, i : i + 1]
+            )
+
+        def join_sums(i):
+            nc.vector.scalar_tensor_tensor(
+                out=part_term[:, i % 2],
+                in0=part_sum[:, i % 2, 0],
+                scalar=1.0,
+                in1=part_sum[:, i % 2, 1],
+                op0=ALU.mult,
+                op1=ALU.mult,
+                accum_out=exp_sum[:, i : i + 1],
+            )
 
         def finish_last(i):
             col = slice(i, i + 1)
-            nc.scalar.activation(out=part_sum[:, 1, :], in_=part[:], func=ACT.Exp, scale=-1.0, bias=neg_max[:, col])
-            nc.vector.scalar_tensor_tensor(
-                out=tail[:, 0, :], in0=part_sum[:, 0, :], scalar=1.0, in1=part_sum[:, 1, :],
-                op0=ALU.mult, op1=ALU.mult, accum_out=tail[:, 1, 0:1],
-            )
-            nc.scalar.activation(out=log_total[:], in_=tail[:, 1, 0:1], func=ACT.Ln)
+            nc.scalar.activation(out=log_total[:], in_=exp_sum[:, col], func=ACT.Ln)
             for c in range(CHUNKS):
                 cols = slice(c * BANK, (c + 1) * BANK)
                 nc.vector.tensor_scalar(
-                    out=logits[i][:, cols], in0=logits[i][:, cols], scalar1=neg_max[:, col], scalar2=log_total[:],
-                    op0=ALU.add, op1=ALU.subtract,
+                    out=logits[i][:, cols],
+                    in0=logits[i][:, cols],
+                    scalar1=neg_max[:, col],
+                    scalar2=log_total[:],
+                    op0=ALU.add,
+                    op1=ALU.subtract,
                 )
                 nc.sync.dma_start(out=logp_rows[:, i, cols], in_=logits[i][:, cols])
 
@@ -333,66 +388,154 @@ def tile_linearvaeitemlogsoftmax_w8_kernel(
                 stage(i, *args)
 
         LAST = TILES - 1
-        for s in range(-3, LAST + 2):
+        spread_bias(0, "z_bank")
+        first_banks = ("t_bank", "t_bank", "t_bank", "x_bank")
+        for k in range(PASSES):
+            widen(0, k, 1, nc.vector.tensor_copy)
+            turn_x(0, k, 1, first_banks[k])
+        for i in (1, 2):
+            for h in (0, 2):
+                widen(i, h)
+        for k in range(PASSES):
+            scale_x(0, k, 1)
+        spread_bias(1, "mu_bank")
+        turn_x(1, 0)
+        turn_x(1, 2)
+        for h in range(2):
+            keep_bias(h)
+        quantize_x(0)
+        encode_lv(0)
+        for h in (0, 2):
+            scale_x(1, h)
+            turn_x(2, h)
+        deviation(0)
+        sample(0)
+        for h in (0, 2):
+            widen(3, h)
+        sum_lv(0)
+        encode_mu(0)
+        copy_mu(0)
+        scale_x(2, 0)
+        turn_x(3, 0)
+        scale_x(2, 2)
+        quantize_x(1)
+        turn_z(0)
+        turn_x(3, 2)
+        encode_lv(1)
+        quantize_x(2)
+        gain_z(0)
+        quantize_z(0)
+        deviation(1)
+        sample(1)
+        decode(0, 0)
+        decode(0, 1)
+        encode_mu(1)
+        decode(0, 2)
+        sum_lv(1)
+        copy_mu(1)
+        widen(4, 0)
+
+        for s in range(2, LAST):
             j = s - 2
-            filling = j < 0
-            run(quantize_x, s)
+            if s > 2:
+                quantize_x(s)
             run(finish, j - 2)
-            if s == TILES:
-                finish_kl()
-            if filling:
-                run(turn_z, j + 1)
-            run(encode_lv, s)
+            if s > 2:
+                encode_lv(s)
             run(sum_exp, j - 1)
             run(log_step, j - 1, 0)
-            run(scale_x, s + 1, 0)
-            run(add_bias, j, 0)
-            run(decode, j, 3)
-            if not filling:
-                run(turn_z, j + 1)
-            run(deviation, s)
+            scale_x(s + 1, 0)
+            add_bias(j, 0)
+            decode(j, 3)
+            turn_z(j + 1)
+            if s == 2:
+                encode_lv(s)
+            deviation(s)
             run(log_step, j - 1, 1)
-            run(sample, s)
-            run(sum_lv, s)
+            sample(s)
+            sum_lv(s)
             run(log_step, j - 1, 2)
+            run(widen, s + 2, 2)
+            run(log_step, j - 1, 3)
             run(turn_x, s + 2, 0)
             for c in range(1, CHUNKS):
-                run(add_bias, j, c)
-            if filling:
-                run(scale_x, s + 1, 1)
-                run(gain_z, j + 1)
-                run(quantize_z, j + 1)
-                for c in range(CHUNKS - 1):
-                    run(decode, j + 1, c)
-                run(encode_mu, s)
-                run(copy_mu, s)
-                run(turn_x, s + 2, 1)
-                run(widen, s + 3, 0)
-                run(widen, s + 3, 1)
-                run(sum_squares, s, 1)
-                run(sum_squares, s, 0)
-            else:
-                run(encode_mu, s)
-                run(gain_z, j + 1)
-                run(scale_x, s + 1, 1)
-                run(quantize_z, j + 1)
-                run(row_max, j)
-                run(turn_x, s + 2, 1)
-                for c in range(CHUNKS - 1):
-                    run(decode, j + 1, c)
-                run(widen, s + 3, 0)
-                run(log_step, j - 1, 3)
-                run(sum_squares, s, 1)
-                run(log_step, j - 1, 4)
-                run(copy_mu, s)
-                run(log_step, j - 1, 5)
-                run(widen, s + 3, 1)
-                run(log_step, j - 1, 6)
-                run(sum_squares, s, 0)
-                run(log_step, j - 1, 7)
-        finish(LAST - 2)
+                add_bias(j, c)
+            encode_mu(s)
+            gain_z(j + 1)
+            scale_x(s + 1, 2)
+            quantize_z(j + 1)
+            row_max(j)
+            run(turn_x, s + 2, 2)
+            for c in range(CHUNKS - 1):
+                decode(j + 1, c)
+            sum_squares(j, 0)
+            run(log_step, j - 1, 4)
+            copy_mu(s)
+            run(log_step, j - 1, 5)
+            run(widen, s + 3, 0)
+            run(log_step, j - 1, 6)
+            sum_squares(j, 1)
+            run(log_step, j - 1, 7)
+            if s == LAST - 1:
+                sum_squares(j + 1, 0)
+                sum_squares(j + 1, 1)
+
+        def logits_step(j):
+            add_bias(j, 0)
+            decode(j, 3)
+            add_bias(j, 1)
+            add_bias(j, 2)
+            gain_z(j + 1)
+            add_bias(j, 3)
+            quantize_z(j + 1)
+            row_max(j)
+
+        quantize_x(LAST)
+        finish(LAST - 4)
+        sum_exp(LAST - 3)
+        sum_squares(LAST - 1, 0)
+        turn_z(LAST - 1)
+        logits_step(LAST - 2)
+        encode_lv(LAST)
+        decode(LAST - 1, 0)
+        encode_mu(LAST)
+        decode(LAST - 1, 1)
+        decode(LAST - 1, 2)
+        log_step(LAST - 3, 0)
+        sum_squares(LAST - 1, 1)
+        for step in range(1, 4):
+            log_step(LAST - 3, step)
+        deviation(LAST)
+        sample(LAST)
+        log_step(LAST - 3, 4)
+        sum_lv(LAST)
+        log_step(LAST - 3, 5)
+        copy_mu(LAST)
+        log_step(LAST - 3, 6)
+        sum_exp(LAST - 2)
+        log_step(LAST - 3, 7)
+        turn_z(LAST)
+        add_bias(LAST - 1, 0)
+        decode(LAST - 1, 3)
+        add_bias(LAST - 1, 1)
+        add_bias(LAST - 1, 2)
+        gain_z(LAST)
+        add_bias(LAST - 1, 3)
+        quantize_z(LAST)
+        finish(LAST - 3)
+        row_max(LAST - 1)
+        for c in range(CHUNKS - 1):
+            decode(LAST, c)
+        log_step(LAST - 2, 0)
+        sum_squares(LAST, 0)
+        log_step(LAST - 2, 1)
+        sum_squares(LAST, 1)
+        for step in range(2, 8):
+            log_step(LAST - 2, step)
         sum_exp(LAST - 1)
         add_bias(LAST, 0)
+        finish(LAST - 2)
+        finish_kl()
         decode(LAST, 3)
         add_bias(LAST, 1)
         chunk_max(LAST, 0)
@@ -403,8 +546,10 @@ def tile_linearvaeitemlogsoftmax_w8_kernel(
         chunk_max(LAST, 3)
         join_max(LAST)
         for c in range(CHUNKS):
-            for step in ((), (0, 1, 2), (3, 4, 5), (6, 7))[c]:
+            for step in ((0,), (1, 2, 3, 4), (5,), (6, 7))[c]:
                 log_step(LAST - 1, step)
             chunk_exp(LAST, c)
         finish_on_vector(LAST - 1)
+        chunk_weights(LAST)
+        join_sums(LAST)
         finish_last(LAST)

@@ -24,7 +24,7 @@ PASSES = I // 512
 BANK = 512
 CHUNKS = I // BANK
 HALF = I // 2
-PSUM_BUFS = {"x_bank": 2, "t_bank": 3, "z_bank": 1}
+PSUM_BUFS = {"x_bank": 2, "t_bank": 4, "mu_bank": 1}
 LN2 = math.log(2.0)
 
 
@@ -82,8 +82,8 @@ def tile_linearvaeitemlogsoftmax_w8_kernel(
             nc.sync.dma_start(out=eps_sb[i // 2][:], in_=eps_rows[:, i : i + 2, :])
 
         load_x(0)
-        nc.sync.dma_start(out=bd_row[0:1, :], in_=bd.rearrange("(o n) -> o n", o=1))
         nc.sync.dma_start(out=x_scale_sb[:], in_=x_scale.rearrange("o (g p t) -> p (o g) t", p=P, t=4))
+        nc.sync.dma_start(out=bd_row[0:1, :], in_=bd.rearrange("(o n) -> o n", o=1))
         load_x(1)
         load_words(wv_sb, wv_words)
         load_scales(1, wv_scales)
@@ -114,7 +114,7 @@ def tile_linearvaeitemlogsoftmax_w8_kernel(
         bias_bank = {}
 
         def spread_bias(h, bank):
-            bias_bank[h] = psum.tile([P, HALF], BF16, name=bank)
+            bias_bank[h] = psum.tile([P, HALF], BF16, name=bank, bufs=PSUM_BUFS[bank])
             for c in range(2):
                 src = slice(h * HALF + c * BANK, h * HALF + (c + 1) * BANK)
                 nc.tensor.matmul(
@@ -137,7 +137,7 @@ def tile_linearvaeitemlogsoftmax_w8_kernel(
 
         def scale_x(i, first, count=2):
             if first == 0:
-                x_grouped[i] = work.tile([P, PASSES, P, 4], BF16, name="x_grouped", align_bytes=64)
+                x_grouped[i] = work.tile([P, PASSES, P, 4], BF16, name="x_grouped", bufs=3, align_bytes=64)
             passes = slice(first, first + count)
             nc.vector.tensor_tensor(
                 out=x_grouped[i][:, passes].rearrange("p g k (u e) -> p g k u e", u=2),
@@ -221,7 +221,7 @@ def tile_linearvaeitemlogsoftmax_w8_kernel(
             )
 
         def turn_z(i):
-            z_bank[i] = psum.tile([P, 4, P], F32, name="z_bank")
+            z_bank[i] = psum.tile([P, 4, P], F32, name="mu_bank")
             for t in range(4):
                 for first, term in ((True, mu_sd[i][:, 0, t, :]), (False, noise[i][:, t, :])):
                     nc.tensor.matmul(
@@ -245,7 +245,7 @@ def tile_linearvaeitemlogsoftmax_w8_kernel(
             )
 
         def decode(i, c):
-            t_bank[i, c] = psum.tile([P, BANK], F32, name="t_bank", bufs=3)
+            t_bank[i, c] = psum.tile([P, BANK], F32, name="t_bank", bufs=4)
             codes, scales = z_mx[i]
             nc.tensor.matmul_mx(
                 out=t_bank[i, c][:],
@@ -388,68 +388,66 @@ def tile_linearvaeitemlogsoftmax_w8_kernel(
                 stage(i, *args)
 
         LAST = TILES - 1
-        spread_bias(0, "z_bank")
-        first_banks = ("t_bank", "t_bank", "t_bank", "x_bank")
+        spread_bias(0, "mu_bank")
         for k in range(PASSES):
             widen(0, k, 1, nc.vector.tensor_copy)
-            turn_x(0, k, 1, first_banks[k])
-        for i in (1, 2):
-            for h in (0, 2):
-                widen(i, h)
-        for k in range(PASSES):
+            turn_x(0, k, 1, "t_bank")
+        for h in range(2):
+            widen(1, 2 * h)
+        for k in range(3):
             scale_x(0, k, 1)
-        spread_bias(1, "mu_bank")
-        turn_x(1, 0)
-        turn_x(1, 2)
+        quantize_x(0, 0, 2)
+        scale_x(0, 3, 1)
+        quantize_x(0, 2, 2)
+        spread_bias(1, "t_bank")
         for h in range(2):
             keep_bias(h)
-        quantize_x(0)
-        encode_lv(0)
         for h in (0, 2):
+            widen(2, h)
+            turn_x(1, h)
+            encode_lv(0, h, 2)
             scale_x(1, h)
-            turn_x(2, h)
         deviation(0)
         sample(0)
+        sum_lv(0)
         for h in (0, 2):
             widen(3, h)
-        sum_lv(0)
-        encode_mu(0)
+            turn_x(2, h)
+            encode_mu(0, h, 2)
         copy_mu(0)
         scale_x(2, 0)
-        turn_x(3, 0)
-        scale_x(2, 2)
         quantize_x(1)
+        scale_x(2, 2)
+        turn_x(3, 0)
+        encode_lv(1, 0, 2)
         turn_z(0)
         turn_x(3, 2)
-        encode_lv(1)
-        quantize_x(2)
+        encode_lv(1, 2, 2)
+        scale_x(3, 0)
         gain_z(0)
+        quantize_x(2)
         quantize_z(0)
+        scale_x(3, 2)
+        encode_mu(1)
+        for c in range(CHUNKS):
+            decode(0, c)
         deviation(1)
         sample(1)
-        decode(0, 0)
-        decode(0, 1)
-        encode_mu(1)
-        decode(0, 2)
         sum_lv(1)
         copy_mu(1)
         widen(4, 0)
+        turn_z(1)
 
         for s in range(2, LAST):
             j = s - 2
-            if s > 2:
+            if s > 3:
                 quantize_x(s)
             run(finish, j - 2)
-            if s > 2:
-                encode_lv(s)
+            encode_lv(s)
             run(sum_exp, j - 1)
             run(log_step, j - 1, 0)
-            scale_x(s + 1, 0)
-            add_bias(j, 0)
-            decode(j, 3)
-            turn_z(j + 1)
-            if s == 2:
-                encode_lv(s)
+            if s > 2:
+                scale_x(s + 1, 0)
             deviation(s)
             run(log_step, j - 1, 1)
             sample(s)
@@ -458,19 +456,28 @@ def tile_linearvaeitemlogsoftmax_w8_kernel(
             run(widen, s + 2, 2)
             run(log_step, j - 1, 3)
             run(turn_x, s + 2, 0)
-            for c in range(1, CHUNKS):
-                add_bias(j, c)
-            encode_mu(s)
+            add_bias(j, 0)
+            add_bias(j, 1)
+            if s == 2:
+                add_bias(j, 2)
+                add_bias(j, 3)
             gain_z(j + 1)
-            scale_x(s + 1, 2)
+            encode_mu(s)
+            if s > 2:
+                add_bias(j, 2)
+                add_bias(j, 3)
+                scale_x(s + 1, 2)
+            else:
+                quantize_x(s + 1)
             quantize_z(j + 1)
             row_max(j)
             run(turn_x, s + 2, 2)
-            for c in range(CHUNKS - 1):
+            for c in range(CHUNKS):
                 decode(j + 1, c)
             sum_squares(j, 0)
             run(log_step, j - 1, 4)
             copy_mu(s)
+            turn_z(s)
             run(log_step, j - 1, 5)
             run(widen, s + 3, 0)
             run(log_step, j - 1, 6)
@@ -480,51 +487,41 @@ def tile_linearvaeitemlogsoftmax_w8_kernel(
                 sum_squares(j + 1, 0)
                 sum_squares(j + 1, 1)
 
-        def logits_step(j):
-            add_bias(j, 0)
-            decode(j, 3)
-            add_bias(j, 1)
-            add_bias(j, 2)
-            gain_z(j + 1)
-            add_bias(j, 3)
-            quantize_z(j + 1)
-            row_max(j)
-
         quantize_x(LAST)
         finish(LAST - 4)
+        encode_lv(LAST)
         sum_exp(LAST - 3)
         sum_squares(LAST - 1, 0)
-        turn_z(LAST - 1)
-        logits_step(LAST - 2)
-        encode_lv(LAST)
-        decode(LAST - 1, 0)
+        gain_z(LAST - 1)
         encode_mu(LAST)
-        decode(LAST - 1, 1)
-        decode(LAST - 1, 2)
+        for c in range(CHUNKS):
+            add_bias(LAST - 2, c)
+        quantize_z(LAST - 1)
+        row_max(LAST - 2)
+        for c in range(CHUNKS):
+            decode(LAST - 1, c)
         log_step(LAST - 3, 0)
-        sum_squares(LAST - 1, 1)
-        for step in range(1, 4):
-            log_step(LAST - 3, step)
         deviation(LAST)
         sample(LAST)
-        log_step(LAST - 3, 4)
-        sum_lv(LAST)
-        log_step(LAST - 3, 5)
+        log_step(LAST - 3, 1)
         copy_mu(LAST)
-        log_step(LAST - 3, 6)
+        turn_z(LAST)
+        log_step(LAST - 3, 2)
+        sum_lv(LAST)
+        log_step(LAST - 3, 3)
+        sum_squares(LAST - 1, 1)
+        for step in range(4, 7):
+            log_step(LAST - 3, step)
         sum_exp(LAST - 2)
         log_step(LAST - 3, 7)
-        turn_z(LAST)
-        add_bias(LAST - 1, 0)
-        decode(LAST - 1, 3)
-        add_bias(LAST - 1, 1)
-        add_bias(LAST - 1, 2)
+        for c in range(CHUNKS - 1):
+            add_bias(LAST - 1, c)
         gain_z(LAST)
         add_bias(LAST - 1, 3)
         quantize_z(LAST)
         finish(LAST - 3)
         row_max(LAST - 1)
-        for c in range(CHUNKS - 1):
+        for c in range(CHUNKS):
             decode(LAST, c)
         log_step(LAST - 2, 0)
         sum_squares(LAST, 0)
@@ -536,7 +533,6 @@ def tile_linearvaeitemlogsoftmax_w8_kernel(
         add_bias(LAST, 0)
         finish(LAST - 2)
         finish_kl()
-        decode(LAST, 3)
         add_bias(LAST, 1)
         chunk_max(LAST, 0)
         add_bias(LAST, 2)
@@ -546,7 +542,7 @@ def tile_linearvaeitemlogsoftmax_w8_kernel(
         chunk_max(LAST, 3)
         join_max(LAST)
         for c in range(CHUNKS):
-            for step in ((0,), (1, 2, 3, 4), (5,), (6, 7))[c]:
+            for step in ((0, 1), (2, 3, 4), (5, 6, 7), ())[c]:
                 log_step(LAST - 1, step)
             chunk_exp(LAST, c)
         finish_on_vector(LAST - 1)

@@ -257,9 +257,16 @@ def tile_linearvaeitemlogsoftmax_w8_kernel(
                 stop=True,
             )
 
+        def copy_chunk(i):
+            logits[i] = work.tile([P, I], F32, name="logits", bufs=6)
+            nc.scalar.copy(out=logits[i][:, :BANK], in_=t_bank[i, 0][:])
+
+        def add_bias_aside(i):
+            nc.gpsimd.tensor_tensor(out=logits[i][:, :BANK], in0=logits[i][:, :BANK], in1=bd_sb[:, :BANK], op=ALU.add)
+
         def add_bias(i, c):
             if c == 0:
-                logits[i] = work.tile([P, I], F32, name="logits", bufs=5)
+                logits[i] = work.tile([P, I], F32, name="logits", bufs=6)
             cols = slice(c * BANK, (c + 1) * BANK)
             nc.vector.tensor_tensor(out=logits[i][:, cols], in0=t_bank[i, c][:], in1=bd_sb[:, cols], op=ALU.add)
 
@@ -319,11 +326,24 @@ def tile_linearvaeitemlogsoftmax_w8_kernel(
                 )
                 nc.sync.dma_start(out=logp_rows[:, i, cols], in_=logits[i][:, cols])
 
+        def sum_squares_on_vector(i):
+            for a in range(2):
+                term = mu_sd[i][:, a].rearrange("p t m -> p (t m)")
+                nc.vector.scalar_tensor_tensor(
+                    out=work.tile([P, Z], BF16, name="unread_by_vector")[:],
+                    in0=term,
+                    scalar=1.0,
+                    in1=term,
+                    op0=ALU.mult,
+                    op1=ALU.mult,
+                    accum_out=sq_sum[:, a, i : i + 1],
+                )
+
         def finish_kl():
             kl = keep.tile([P, TILES], F32)
-            nc.gpsimd.tensor_tensor(out=kl[:], in0=sq_sum[:, 1], in1=lv_sum[:], op=ALU.subtract)
-            nc.gpsimd.tensor_tensor(out=kl[:], in0=kl[:], in1=sq_sum[:, 0], op=ALU.add)
-            nc.gpsimd.tensor_scalar(out=kl[:], in0=kl[:], scalar1=0.5 / Z, scalar2=-0.5, op0=ALU.mult, op1=ALU.add)
+            nc.vector.tensor_tensor(out=kl[:], in0=sq_sum[:, 1], in1=lv_sum[:], op=ALU.subtract)
+            nc.vector.tensor_tensor(out=kl[:], in0=kl[:], in1=sq_sum[:, 0], op=ALU.add)
+            nc.vector.tensor_scalar(out=kl[:], in0=kl[:], scalar1=0.5 / Z, scalar2=-0.5, op0=ALU.mult, op1=ALU.add)
             nc.sync.dma_start(out=out_1.rearrange("(p i) -> p i", i=TILES), in_=kl[:])
 
         part_max = keep.tile([P, 2, CHUNKS], F32)
@@ -438,7 +458,7 @@ def tile_linearvaeitemlogsoftmax_w8_kernel(
         widen(4, 0)
         turn_z(1)
 
-        for s in range(2, LAST):
+        for s in range(2, 3):
             j = s - 2
             if s > 3:
                 quantize_x(s)
@@ -483,15 +503,55 @@ def tile_linearvaeitemlogsoftmax_w8_kernel(
             run(log_step, j - 1, 6)
             sum_squares(j, 1)
             run(log_step, j - 1, 7)
-            if s == LAST - 1:
-                sum_squares(j + 1, 0)
-                sum_squares(j + 1, 1)
+
+        for s in range(3, LAST):
+            j = s - 2
+            aside = 2 <= j + 1 <= 4
+            scale_x(s + 1, 0)
+            if not 2 <= j <= 4:
+                add_bias(j, 0)
+            gain_z(j + 1)
+            if s > 3:
+                quantize_x(s)
+            quantize_z(j + 1)
+            run(finish, j - 2)
+            run(turn_x, s + 2, 0)
+            encode_lv(s)
+            decode(j + 1, 0)
+            encode_mu(s)
+            sum_exp(j - 1)
+            log_step(j - 1, 0)
+            run(widen, s + 2, 2)
+            log_step(j - 1, 1)
+            deviation(s)
+            sample(s)
+            log_step(j - 1, 2)
+            if aside:
+                copy_chunk(j + 1)
+                add_bias_aside(j + 1)
+            log_step(j - 1, 3)
+            copy_mu(s)
+            log_step(j - 1, 4)
+            sum_lv(s)
+            log_step(j - 1, 5)
+            sum_squares(j, 0)
+            log_step(j - 1, 6)
+            for c in range(1, CHUNKS):
+                add_bias(j, c)
+            scale_x(s + 1, 2)
+            row_max(j)
+            run(turn_x, s + 2, 2)
+            turn_z(s)
+            for c in range(1, CHUNKS):
+                decode(j + 1, c)
+            run(widen, s + 3, 0)
+            log_step(j - 1, 7)
+            sum_squares(j, 1)
 
         quantize_x(LAST)
         finish(LAST - 4)
         encode_lv(LAST)
         sum_exp(LAST - 3)
-        sum_squares(LAST - 1, 0)
         gain_z(LAST - 1)
         encode_mu(LAST)
         for c in range(CHUNKS):
@@ -500,20 +560,20 @@ def tile_linearvaeitemlogsoftmax_w8_kernel(
         row_max(LAST - 2)
         for c in range(CHUNKS):
             decode(LAST - 1, c)
-        log_step(LAST - 3, 0)
+        for step in range(2):
+            log_step(LAST - 3, step)
+            sum_squares(LAST - 2, step)
+        log_step(LAST - 3, 2)
         deviation(LAST)
         sample(LAST)
-        log_step(LAST - 3, 1)
+        log_step(LAST - 3, 3)
         copy_mu(LAST)
         turn_z(LAST)
-        log_step(LAST - 3, 2)
+        log_step(LAST - 3, 4)
         sum_lv(LAST)
-        log_step(LAST - 3, 3)
-        sum_squares(LAST - 1, 1)
-        for step in range(4, 7):
+        for step in range(5, 8):
             log_step(LAST - 3, step)
         sum_exp(LAST - 2)
-        log_step(LAST - 3, 7)
         for c in range(CHUNKS - 1):
             add_bias(LAST - 1, c)
         gain_z(LAST)
@@ -523,17 +583,14 @@ def tile_linearvaeitemlogsoftmax_w8_kernel(
         row_max(LAST - 1)
         for c in range(CHUNKS):
             decode(LAST, c)
-        log_step(LAST - 2, 0)
-        sum_squares(LAST, 0)
-        log_step(LAST - 2, 1)
-        sum_squares(LAST, 1)
-        for step in range(2, 8):
+        for step in range(8):
             log_step(LAST - 2, step)
+            if step < 2:
+                sum_squares(LAST - 1, step)
         sum_exp(LAST - 1)
         add_bias(LAST, 0)
-        finish(LAST - 2)
-        finish_kl()
         add_bias(LAST, 1)
+        finish(LAST - 2)
         chunk_max(LAST, 0)
         add_bias(LAST, 2)
         chunk_max(LAST, 1)
@@ -548,4 +605,6 @@ def tile_linearvaeitemlogsoftmax_w8_kernel(
         finish_on_vector(LAST - 1)
         chunk_weights(LAST)
         join_sums(LAST)
+        sum_squares_on_vector(LAST)
         finish_last(LAST)
+        finish_kl()

@@ -19,13 +19,27 @@ ACT = mybir.ActivationFunctionType
 AXIS = mybir.AxisListType
 
 P = 128
+PACK = 4
+K_PASS = P * PACK
 TILES = N // P
-PASSES = I // 512
+LAST = TILES - 1
+PASSES = I // K_PASS
+HALVES = (0, 2)
 BANK = 512
 CHUNKS = I // BANK
 HALF = I // 2
-PSUM_BUFS = {"x_bank": 2, "t_bank": 4, "mu_bank": 1}
 LN2 = math.log(2.0)
+LOG_STEPS = 8
+
+PSUM_BUFS = {"x_bank": 2, "t_bank": 4, "mu_bank": 1}
+WM_SLOT, WV_SLOT, WD_SLOT = 0, 1, 2
+WIDE_BUFS = 8
+GROUPED_BUFS = 3
+MU_SD_BUFS = 4
+NOISE_BUFS = 3
+LOGITS_BUFS = 6
+BIAS_ASIDE = range(2, 5)
+VECTOR_WIDENS = range(5, 7)
 
 
 def tile_linearvaeitemlogsoftmax_w8_kernel(
@@ -56,45 +70,44 @@ def tile_linearvaeitemlogsoftmax_w8_kernel(
         minus_3_halves, minus_one, minus_two = (consts[:, col : col + 1] for col in range(3))
 
         x_sb = [keep.tile([P, I], U8, name="x_codes_%d" % i) for i in range(TILES)]
-        x_scale_sb = keep.tile([P, PASSES, 4], F32)
+        x_scale_sb = keep.tile([P, PASSES, PACK], F32)
         wm_sb = keep.tile([P, PASSES, Z], U32, align_bytes=64)
         wv_sb = keep.tile([P, PASSES, Z], U32, align_bytes=64)
         wd_sb = keep.tile([P, I], U32, align_bytes=64)
-        eps_sb = [keep.tile([P, 2, Z], BF16, name="eps_%d" % h) for h in range(TILES // 2)]
-        g_sb = keep.tile([P, 4], BF16)
+        eps_sb = [keep.tile([P, 2, Z], BF16, name="eps_%d" % pair) for pair in range(TILES // 2)]
+        g_sb = keep.tile([P, PACK], BF16)
         bd_sb = keep.tile([P, I], BF16)
 
         def load_x(i):
             nc.sync.dma_start(out=x_sb[i][:], in_=x_rows[:, i, :])
 
         def load_scales(slot, rows):
-            for q in range(4):
+            for quad in range(4):
                 nc.sync.dma_start(
-                    out=w_scales[32 * q : 32 * q + 16, slot, :].bitcast(I32),
-                    in_=rows[:, 4 * q : 4 * q + 4, :].bitcast(I32),
+                    out=w_scales[32 * quad : 32 * quad + 16, slot, :].bitcast(I32),
+                    in_=rows[:, 4 * quad : 4 * quad + 4, :].bitcast(I32),
                 )
 
         def load_words(dst, words):
-            src = words.rearrange("g p n t -> p g (n t)").bitcast(I32)
-            nc.sync.dma_start(out=dst[:].bitcast(I32), in_=src)
+            nc.sync.dma_start(out=dst[:].bitcast(I32), in_=words.rearrange("c p n t -> p c (n t)").bitcast(I32))
 
         def load_eps(i):
             nc.sync.dma_start(out=eps_sb[i // 2][:], in_=eps_rows[:, i : i + 2, :])
 
         load_x(0)
-        nc.sync.dma_start(out=x_scale_sb[:], in_=x_scale.rearrange("o (g p t) -> p (o g) t", p=P, t=4))
+        nc.sync.dma_start(out=x_scale_sb[:], in_=x_scale.rearrange("o (c p t) -> p (o c) t", p=P, t=PACK))
         nc.sync.dma_start(out=bd_row[0:1, :], in_=bd.rearrange("(o n) -> o n", o=1))
         load_x(1)
         load_words(wv_sb, wv_words)
-        load_scales(1, wv_scales)
+        load_scales(WV_SLOT, wv_scales)
         load_x(2)
         load_words(wm_sb, wm_words)
         load_eps(0)
-        load_scales(0, wm_scales)
+        load_scales(WM_SLOT, wm_scales)
         load_x(3)
         nc.sync.dma_start(out=wd_sb[:].bitcast(I32), in_=wd_words[0].rearrange("p n t -> p (n t)").bitcast(I32))
-        nc.sync.dma_start(out=g_sb[:], in_=g.rearrange("(p t) -> p t", t=4))
-        load_scales(2, wd_scales[0].rearrange("r (c n) -> c r n", n=BANK))
+        nc.sync.dma_start(out=g_sb[:], in_=g.rearrange("(p t) -> p t", t=PACK))
+        load_scales(WD_SLOT, wd_scales[0].rearrange("r (c n) -> c r n", n=BANK))
         for i in range(4, TILES):
             load_x(i)
             if i % 2 == 0:
@@ -106,52 +119,55 @@ def tile_linearvaeitemlogsoftmax_w8_kernel(
         exp_sum = keep.tile([P, TILES], F32)
         lv_sum = keep.tile([P, TILES], F32)
         sq_sum = keep.tile([P, 2, TILES], F32)
-        log_steps = keep.tile([P, 8, TILES], F32)
+        log_state = keep.tile([P, LOG_STEPS, TILES], F32)
+        chunk_neg_max = keep.tile([P, CHUNKS], F32)
+        chunk_sum = keep.tile([P, 2, CHUNKS], F32)
+        chunk_term = keep.tile([P, CHUNKS], F32)
+        log_total = keep.tile([P, 1], F32)
 
-        wide, x_bank, x_grouped, x_mx, lv_bank, mu_bank, mu_sd, noise = {}, {}, {}, {}, {}, {}, {}, {}
-        z_bank, z_grouped, z_mx, t_bank, logits = {}, {}, {}, {}, {}
+        bias_bank, wide, x_bank, x_grouped, x_mx, lv_bank, mu_bank, mu_sd = {}, {}, {}, {}, {}, {}, {}, {}
+        noise, z_bank, z_grouped, z_mx, t_bank, logits = {}, {}, {}, {}, {}, {}
 
-        bias_bank = {}
+        def psum_tile(shape, dtype, bank):
+            return psum.tile(shape, dtype, name=bank, bufs=PSUM_BUFS[bank])
 
-        def spread_bias(h, bank):
-            bias_bank[h] = psum.tile([P, HALF], BF16, name=bank, bufs=PSUM_BUFS[bank])
+        def spread_bias(half, bank):
+            bias_bank[half] = psum_tile([P, HALF], BF16, bank)
             for c in range(2):
-                src = slice(h * HALF + c * BANK, h * HALF + (c + 1) * BANK)
-                nc.tensor.matmul(
-                    out=bias_bank[h][:, c * BANK : (c + 1) * BANK], lhsT=ones[:], rhs=bd_row[:, src], start=True, stop=True
-                )
+                src = slice(half * HALF + c * BANK, half * HALF + (c + 1) * BANK)
+                dst = bias_bank[half][:, c * BANK : (c + 1) * BANK]
+                nc.tensor.matmul(out=dst, lhsT=ones[:], rhs=bd_row[:, src], start=True, stop=True)
 
-        def keep_bias(h):
-            nc.scalar.copy(out=bd_sb[:, h * HALF : (h + 1) * HALF], in_=bias_bank[h][:])
+        def keep_bias(half):
+            nc.scalar.copy(out=bd_sb[:, half * HALF : (half + 1) * HALF], in_=bias_bank[half][:])
 
         def widen(i, first, count=2, copy=nc.scalar.copy):
-            wide[i, first] = work.tile([P, count * BANK], BF16, name="wide", bufs=8)
-            copy(out=wide[i, first][:], in_=x_sb[i][:, first * BANK : (first + count) * BANK].bitcast(FP8))
+            wide[i, first] = work.tile([P, count * K_PASS], BF16, name="wide", bufs=WIDE_BUFS)
+            copy(out=wide[i, first][:], in_=x_sb[i][:, first * K_PASS : (first + count) * K_PASS].bitcast(FP8))
 
         def turn_x(i, first, count=2, bank="x_bank"):
-            x_bank[i, first] = psum.tile([P, 2, count, P], F32, name=bank, bufs=PSUM_BUFS[bank])
+            x_bank[i, first] = psum_tile([P, 2, count, P], F32, bank)
             words = wide[i, first][:].bitcast(F32)
-            for k in range(count):
+            for c in range(count):
                 for u in range(2):
-                    nc.tensor.transpose(x_bank[i, first][:, u, k, :], words[:, 256 * k + u : 256 * (k + 1) : 2], ident[:])
+                    every_second = words[:, 2 * P * c + u : 2 * P * (c + 1) : 2]
+                    nc.tensor.transpose(x_bank[i, first][:, u, c, :], every_second, ident[:])
 
         def scale_x(i, first, count=2):
             if first == 0:
-                x_grouped[i] = work.tile([P, PASSES, P, 4], BF16, name="x_grouped", bufs=3, align_bytes=64)
+                x_grouped[i] = work.tile([P, PASSES, P, PACK], BF16, name="x_grouped", bufs=GROUPED_BUFS, align_bytes=64)
             passes = slice(first, first + count)
+            scale = x_scale_sb[:, passes, :].rearrange("p c (u e) -> p c u e", u=2)
             nc.vector.tensor_tensor(
-                out=x_grouped[i][:, passes].rearrange("p g k (u e) -> p g k u e", u=2),
-                in0=x_bank[i, first][:].bitcast(BF16).rearrange("p u g (k e) -> p g k u e", e=2),
-                in1=x_scale_sb[:, passes, :]
-                .rearrange("p g (u e) -> p g u e", u=2)
-                .unsqueeze(2)
-                .broadcast_to([P, count, P, 2, 2]),
+                out=x_grouped[i][:, passes].rearrange("p c n (u e) -> p c n u e", u=2),
+                in0=x_bank[i, first][:].bitcast(BF16).rearrange("p u c (n e) -> p c n u e", e=2),
+                in1=scale.unsqueeze(2).broadcast_to([P, count, P, 2, 2]),
                 op=ALU.mult,
             )
 
-        def mx_tiles(name, words):
-            codes = work.tile([P, words], U32, name=name + "_codes", align_bytes=64)
-            scales = work.tile([P, words], U8, name=name + "_scales", align_bytes=64)
+        def mx_tiles(name, columns):
+            codes = work.tile([P, columns], U32, name=name + "_codes", align_bytes=64)
+            scales = work.tile([P, columns], U8, name=name + "_scales", align_bytes=64)
             return codes, scales
 
         def quantize_x(i, first=0, count=PASSES):
@@ -162,78 +178,92 @@ def tile_linearvaeitemlogsoftmax_w8_kernel(
             nc.vector.quantize_mx(
                 out=codes[:, cols].bitcast(FP8X4),
                 scales=scales[:, cols],
-                in_=x_grouped[i][:, first : first + count].rearrange("p g k t -> p (g k t)"),
+                in_=x_grouped[i][:, first : first + count].rearrange("p c n t -> p (c n t)"),
             )
 
         def encode(i, bank, w_sb, slot, passes):
             codes, scales = x_mx[i]
-            for k in passes:
-                cols = slice(k * P, (k + 1) * P)
+            for c in passes:
+                cols = slice(c * P, (c + 1) * P)
                 nc.tensor.matmul_mx(
                     out=bank[:],
                     lhsT=codes[:, cols].bitcast(FP8X4),
                     lhsT_scale=scales[:, cols],
-                    rhs=w_sb[:, k, :].bitcast(FP8X4),
-                    rhs_scale=w_scales[4 * k :, slot, :],
-                    start=(k == 0),
-                    stop=(k == PASSES - 1),
+                    rhs=w_sb[:, c, :].bitcast(FP8X4),
+                    rhs_scale=w_scales[4 * c :, slot, :],
+                    start=(c == 0),
+                    stop=(c == PASSES - 1),
                 )
 
         def encode_lv(i, first=0, count=PASSES):
             if first == 0:
                 lv_bank[i] = psum.tile([P, Z], F32, name="lv_bank")
-            encode(i, lv_bank[i], wv_sb, 1, range(first, first + count))
+            encode(i, lv_bank[i], wv_sb, WV_SLOT, range(first, first + count))
 
         def encode_mu(i, first=0, count=PASSES):
             if first == 0:
-                mu_bank[i] = psum.tile([P, Z], F32, name="mu_bank")
-            encode(i, mu_bank[i], wm_sb, 0, range(first, first + count))
+                mu_bank[i] = psum_tile([P, Z], F32, "mu_bank")
+            encode(i, mu_bank[i], wm_sb, WM_SLOT, range(first, first + count))
 
-        def by_slot(ap):
-            return ap.rearrange("p (m t) -> p t m", t=4)
+        def by_byte(ap):
+            return ap.rearrange("p (m t) -> p t m", t=PACK)
 
         def unread(width):
             scratch = work.tile([P, I], BF16, name="unread")
             return scratch[:, :width]
 
         def deviation(i):
-            mu_sd[i] = work.tile([P, 2, 4, P], F32, name="mu_sd", bufs=4)
-            nc.scalar.activation(out=mu_sd[i][:, 1], in_=by_slot(lv_bank[i][:]), func=ACT.Exp, scale=0.5)
+            mu_sd[i] = work.tile([P, 2, PACK, P], F32, name="mu_sd", bufs=MU_SD_BUFS)
+            nc.scalar.activation(out=mu_sd[i][:, 1], in_=by_byte(lv_bank[i][:]), func=ACT.Exp, scale=0.5)
 
         def sum_lv(i):
             nc.scalar.activation(out=unread(Z), in_=lv_bank[i][:], func=ACT.Identity, accum_out=lv_sum[:, i : i + 1])
 
         def copy_mu(i):
-            nc.scalar.copy(out=mu_sd[i][:, 0], in_=by_slot(mu_bank[i][:]))
+            nc.scalar.copy(out=mu_sd[i][:, 0], in_=by_byte(mu_bank[i][:]))
 
-        def sum_squares(i, a):
+        def sum_squares(i, term):
             nc.scalar.activation(
                 out=unread(Z),
-                in_=mu_sd[i][:, a].rearrange("p t m -> p (t m)"),
+                in_=mu_sd[i][:, term].rearrange("p t m -> p (t m)"),
                 func=ACT.Square,
-                accum_out=sq_sum[:, a, i : i + 1],
+                accum_out=sq_sum[:, term, i : i + 1],
             )
 
+        def sum_squares_on_vector(i):
+            for term in range(2):
+                values = mu_sd[i][:, term].rearrange("p t m -> p (t m)")
+                scratch = work.tile([P, Z], BF16, name="unread_of_vector")
+                nc.vector.scalar_tensor_tensor(
+                    out=scratch[:],
+                    in0=values,
+                    scalar=1.0,
+                    in1=values,
+                    op0=ALU.mult,
+                    op1=ALU.mult,
+                    accum_out=sq_sum[:, term, i : i + 1],
+                )
+
         def sample(i):
-            noise[i] = work.tile([P, 4, P], F32, name="noise", bufs=3)
+            noise[i] = work.tile([P, PACK, P], F32, name="noise", bufs=NOISE_BUFS)
             nc.gpsimd.tensor_tensor(
-                out=noise[i][:], in0=mu_sd[i][:, 1], in1=by_slot(eps_sb[i // 2][:, i % 2, :]), op=ALU.mult
+                out=noise[i][:], in0=mu_sd[i][:, 1], in1=by_byte(eps_sb[i // 2][:, i % 2, :]), op=ALU.mult
             )
 
         def turn_z(i):
-            z_bank[i] = psum.tile([P, 4, P], F32, name="mu_bank")
-            for t in range(4):
-                for first, term in ((True, mu_sd[i][:, 0, t, :]), (False, noise[i][:, t, :])):
+            z_bank[i] = psum_tile([P, PACK, P], F32, "mu_bank")
+            for t in range(PACK):
+                for opens, term in ((True, mu_sd[i][:, 0, t, :]), (False, noise[i][:, t, :])):
                     nc.tensor.matmul(
-                        out=z_bank[i][:, t, :], lhsT=term, rhs=ident[:], is_transpose=True, start=first, stop=not first
+                        out=z_bank[i][:, t, :], lhsT=term, rhs=ident[:], is_transpose=True, start=opens, stop=not opens
                     )
 
         def gain_z(i):
-            z_grouped[i] = work.tile([P, P, 4], BF16, name="z_grouped", align_bytes=64)
+            z_grouped[i] = work.tile([P, P, PACK], BF16, name="z_grouped", align_bytes=64)
             nc.vector.tensor_tensor(
                 out=z_grouped[i][:],
-                in0=z_bank[i][:].rearrange("p t k -> p k t"),
-                in1=g_sb[:].unsqueeze(1).broadcast_to([P, P, 4]),
+                in0=z_bank[i][:].rearrange("p t n -> p n t"),
+                in1=g_sb[:].unsqueeze(1).broadcast_to([P, P, PACK]),
                 op=ALU.mult,
             )
 
@@ -241,34 +271,36 @@ def tile_linearvaeitemlogsoftmax_w8_kernel(
             z_mx[i] = mx_tiles("zq", P)
             codes, scales = z_mx[i]
             nc.vector.quantize_mx(
-                out=codes[:].bitcast(FP8X4), scales=scales[:], in_=z_grouped[i][:].rearrange("p k t -> p (k t)")
+                out=codes[:].bitcast(FP8X4), scales=scales[:], in_=z_grouped[i][:].rearrange("p n t -> p (n t)")
             )
 
         def decode(i, c):
-            t_bank[i, c] = psum.tile([P, BANK], F32, name="t_bank", bufs=4)
+            t_bank[i, c] = psum_tile([P, BANK], F32, "t_bank")
             codes, scales = z_mx[i]
             nc.tensor.matmul_mx(
                 out=t_bank[i, c][:],
                 lhsT=codes[:].bitcast(FP8X4),
                 lhsT_scale=scales[:],
                 rhs=wd_sb[:, c * BANK : (c + 1) * BANK].bitcast(FP8X4),
-                rhs_scale=w_scales[4 * c :, 2, :],
+                rhs_scale=w_scales[4 * c :, WD_SLOT, :],
                 start=True,
                 stop=True,
             )
 
-        def copy_chunk(i):
-            logits[i] = work.tile([P, I], F32, name="logits", bufs=6)
-            nc.scalar.copy(out=logits[i][:, :BANK], in_=t_bank[i, 0][:])
-
-        def add_bias_aside(i):
-            nc.gpsimd.tensor_tensor(out=logits[i][:, :BANK], in0=logits[i][:, :BANK], in1=bd_sb[:, :BANK], op=ALU.add)
+        def new_logits(i):
+            logits[i] = work.tile([P, I], F32, name="logits", bufs=LOGITS_BUFS)
 
         def add_bias(i, c):
             if c == 0:
-                logits[i] = work.tile([P, I], F32, name="logits", bufs=6)
+                new_logits(i)
             cols = slice(c * BANK, (c + 1) * BANK)
             nc.vector.tensor_tensor(out=logits[i][:, cols], in0=t_bank[i, c][:], in1=bd_sb[:, cols], op=ALU.add)
+
+        def add_bias_aside(i):
+            new_logits(i)
+            chunk = logits[i][:, :BANK]
+            nc.scalar.copy(out=chunk, in_=t_bank[i, 0][:])
+            nc.gpsimd.tensor_tensor(out=chunk, in0=chunk, in1=bd_sb[:, :BANK], op=ALU.add)
 
         def row_max(i):
             nc.vector.tensor_reduce(out=neg_max[:, i : i + 1], in_=logits[i][:], axis=AXIS.X, op=ALU.max, negate=True)
@@ -284,60 +316,71 @@ def tile_linearvaeitemlogsoftmax_w8_kernel(
 
         def log_step(i, step):
             total = exp_sum[:, i : i + 1]
-            u0, e0, q, u1, e1, u2, e2, y = (log_steps[:, row, i : i + 1] for row in range(8))
-            if step == 0:
-                nc.scalar.activation(
-                    out=u0, in_=total.bitcast(U32), func=ACT.Copy, scale=LN2 / 2**23, bias=(0.043 - 127.0) * LN2 - 1.5
-                )
-            elif step == 1:
-                nc.scalar.activation(out=e0, in_=u0, func=ACT.Exp, scale=-1.0, bias=minus_3_halves)
-            elif step == 2:
-                nc.scalar.activation(out=q, in_=e0, func=ACT.Square, scale=total, bias=minus_two)
-            elif step == 3:
-                nc.scalar.activation(out=u1, in_=q, func=ACT.Identity, scale=-0.5, bias=u0)
-            elif step == 4:
-                nc.scalar.activation(out=e1, in_=u1, func=ACT.Exp, scale=-1.0, bias=minus_two)
-            elif step == 5:
-                nc.scalar.activation(out=u2, in_=e1, func=ACT.Identity, scale=total, bias=u1)
-            elif step == 6:
-                nc.scalar.activation(out=e2, in_=u2, func=ACT.Exp, scale=-1.0, bias=minus_one)
-            else:
-                nc.scalar.activation(out=y, in_=e2, func=ACT.Identity, scale=total, bias=u2)
+            u0, e0, square, u1, e1, u2, e2, u3 = (log_state[:, row, i : i + 1] for row in range(LOG_STEPS))
+            out, in_, func, scale, bias = (
+                (u0, total.bitcast(U32), ACT.Copy, LN2 / 2**23, (0.043 - 127.0) * LN2 - 1.5),
+                (e0, u0, ACT.Exp, -1.0, minus_3_halves),
+                (square, e0, ACT.Square, total, minus_two),
+                (u1, square, ACT.Identity, -0.5, u0),
+                (e1, u1, ACT.Exp, -1.0, minus_two),
+                (u2, e1, ACT.Identity, total, u1),
+                (e2, u2, ACT.Exp, -1.0, minus_one),
+                (u3, e2, ACT.Identity, total, u2),
+            )[step]
+            nc.scalar.activation(out=out, in_=in_, func=func, scale=scale, bias=bias)
+
+        def log_sum(i):
+            return log_state[:, LOG_STEPS - 1, i : i + 1]
 
         def finish(i):
             col = slice(i, i + 1)
-            nc.vector.tensor_tensor(out=neg_lse[:, col], in0=neg_max[:, col], in1=log_steps[:, 7, col], op=ALU.subtract)
+            nc.vector.tensor_tensor(out=neg_lse[:, col], in0=neg_max[:, col], in1=log_sum(i), op=ALU.subtract)
             nc.gpsimd.tensor_scalar(
                 out=logits[i][:], in0=logits[i][:], scalar1=1.0, scalar2=neg_lse[:, col], op0=ALU.mult, op1=ALU.add
             )
             nc.sync.dma_start(out=logp_rows[:, i, :], in_=logits[i][:])
 
-        def finish_on_vector(i):
-            col = slice(i, i + 1)
-            for h in range(2):
-                cols = slice(h * HALF, (h + 1) * HALF)
+        def finish_on_vector(i, log_of_sum, width):
+            for start in range(0, I, width):
+                cols = slice(start, start + width)
                 nc.vector.tensor_scalar(
                     out=logits[i][:, cols],
                     in0=logits[i][:, cols],
-                    scalar1=neg_max[:, col],
-                    scalar2=log_steps[:, 7, col],
+                    scalar1=neg_max[:, i : i + 1],
+                    scalar2=log_of_sum,
                     op0=ALU.add,
                     op1=ALU.subtract,
                 )
                 nc.sync.dma_start(out=logp_rows[:, i, cols], in_=logits[i][:, cols])
 
-        def sum_squares_on_vector(i):
-            for a in range(2):
-                term = mu_sd[i][:, a].rearrange("p t m -> p (t m)")
-                nc.vector.scalar_tensor_tensor(
-                    out=work.tile([P, Z], BF16, name="unread_by_vector")[:],
-                    in0=term,
-                    scalar=1.0,
-                    in1=term,
-                    op0=ALU.mult,
-                    op1=ALU.mult,
-                    accum_out=sq_sum[:, a, i : i + 1],
-                )
+        def chunk_max(c):
+            cols = slice(c * BANK, (c + 1) * BANK)
+            nc.vector.tensor_reduce(
+                out=chunk_neg_max[:, c : c + 1], in_=logits[LAST][:, cols], axis=AXIS.X, op=ALU.max, negate=True
+            )
+
+        def chunk_exp(c):
+            nc.scalar.activation(
+                out=unread(BANK),
+                in_=logits[LAST][:, c * BANK : (c + 1) * BANK],
+                func=ACT.Exp,
+                bias=chunk_neg_max[:, c : c + 1],
+                accum_out=chunk_sum[:, 0, c : c + 1],
+            )
+
+        def join_chunks():
+            nc.scalar.activation(
+                out=chunk_sum[:, 1], in_=chunk_neg_max[:], func=ACT.Exp, scale=-1.0, bias=neg_max[:, LAST:]
+            )
+            nc.vector.scalar_tensor_tensor(
+                out=chunk_term[:],
+                in0=chunk_sum[:, 0],
+                scalar=1.0,
+                in1=chunk_sum[:, 1],
+                op0=ALU.mult,
+                op1=ALU.mult,
+                accum_out=exp_sum[:, LAST:],
+            )
 
         def finish_kl():
             kl = keep.tile([P, TILES], F32)
@@ -346,94 +389,36 @@ def tile_linearvaeitemlogsoftmax_w8_kernel(
             nc.vector.tensor_scalar(out=kl[:], in0=kl[:], scalar1=0.5 / Z, scalar2=-0.5, op0=ALU.mult, op1=ALU.add)
             nc.sync.dma_start(out=out_1.rearrange("(p i) -> p i", i=TILES), in_=kl[:])
 
-        part_max = keep.tile([P, 2, CHUNKS], F32)
-        part_sum = keep.tile([P, 2, 2, CHUNKS], F32)
-        part_term = keep.tile([P, 2, CHUNKS], F32)
-        log_total = keep.tile([P, 1], F32)
-
-        def chunk_max(i, c):
-            nc.vector.tensor_reduce(
-                out=part_max[:, i % 2, c : c + 1],
-                in_=logits[i][:, c * BANK : (c + 1) * BANK],
-                axis=AXIS.X,
-                op=ALU.max,
-                negate=True,
-            )
-
-        def chunk_exp(i, c):
-            nc.scalar.activation(
-                out=unread(BANK),
-                in_=logits[i][:, c * BANK : (c + 1) * BANK],
-                func=ACT.Exp,
-                bias=part_max[:, i % 2, c : c + 1],
-                accum_out=part_sum[:, i % 2, 0, c : c + 1],
-            )
-
-        def join_max(i):
-            nc.vector.tensor_reduce(out=neg_max[:, i : i + 1], in_=part_max[:, i % 2], axis=AXIS.X, op=ALU.min)
-
-        def chunk_weights(i):
-            nc.scalar.activation(
-                out=part_sum[:, i % 2, 1], in_=part_max[:, i % 2], func=ACT.Exp, scale=-1.0, bias=neg_max[:, i : i + 1]
-            )
-
-        def join_sums(i):
-            nc.vector.scalar_tensor_tensor(
-                out=part_term[:, i % 2],
-                in0=part_sum[:, i % 2, 0],
-                scalar=1.0,
-                in1=part_sum[:, i % 2, 1],
-                op0=ALU.mult,
-                op1=ALU.mult,
-                accum_out=exp_sum[:, i : i + 1],
-            )
-
-        def finish_last(i):
-            col = slice(i, i + 1)
-            nc.scalar.activation(out=log_total[:], in_=exp_sum[:, col], func=ACT.Ln)
-            for c in range(CHUNKS):
-                cols = slice(c * BANK, (c + 1) * BANK)
-                nc.vector.tensor_scalar(
-                    out=logits[i][:, cols],
-                    in0=logits[i][:, cols],
-                    scalar1=neg_max[:, col],
-                    scalar2=log_total[:],
-                    op0=ALU.add,
-                    op1=ALU.subtract,
-                )
-                nc.sync.dma_start(out=logp_rows[:, i, cols], in_=logits[i][:, cols])
-
-        def run(stage, i, *args, end=TILES):
-            if 0 <= i < end:
+        def run(stage, i, *args):
+            if 0 <= i < TILES:
                 stage(i, *args)
 
-        LAST = TILES - 1
         spread_bias(0, "mu_bank")
-        for k in range(PASSES):
-            widen(0, k, 1, nc.vector.tensor_copy)
-            turn_x(0, k, 1, "t_bank")
-        for h in range(2):
-            widen(1, 2 * h)
-        for k in range(3):
-            scale_x(0, k, 1)
+        for c in range(PASSES):
+            widen(0, c, 1, nc.vector.tensor_copy)
+            turn_x(0, c, 1, "t_bank")
+        for first in HALVES:
+            widen(1, first)
+        for c in range(PASSES - 1):
+            scale_x(0, c, 1)
         quantize_x(0, 0, 2)
-        scale_x(0, 3, 1)
+        scale_x(0, PASSES - 1, 1)
         quantize_x(0, 2, 2)
         spread_bias(1, "t_bank")
-        for h in range(2):
-            keep_bias(h)
-        for h in (0, 2):
-            widen(2, h)
-            turn_x(1, h)
-            encode_lv(0, h, 2)
-            scale_x(1, h)
+        for half in range(2):
+            keep_bias(half)
+        for first in HALVES:
+            widen(2, first)
+            turn_x(1, first)
+            encode_lv(0, first, 2)
+            scale_x(1, first)
         deviation(0)
         sample(0)
         sum_lv(0)
-        for h in (0, 2):
-            widen(3, h)
-            turn_x(2, h)
-            encode_mu(0, h, 2)
+        for first in HALVES:
+            widen(3, first)
+            turn_x(2, first)
+            encode_mu(0, first, 2)
         copy_mu(0)
         scale_x(2, 0)
         quantize_x(1)
@@ -458,62 +443,41 @@ def tile_linearvaeitemlogsoftmax_w8_kernel(
         widen(4, 0)
         turn_z(1)
 
-        for s in range(2, 3):
-            j = s - 2
-            if s > 3:
-                quantize_x(s)
-            run(finish, j - 2)
-            encode_lv(s)
-            run(sum_exp, j - 1)
-            run(log_step, j - 1, 0)
-            if s > 2:
-                scale_x(s + 1, 0)
-            deviation(s)
-            run(log_step, j - 1, 1)
-            sample(s)
-            sum_lv(s)
-            run(log_step, j - 1, 2)
-            run(widen, s + 2, 2)
-            run(log_step, j - 1, 3)
-            run(turn_x, s + 2, 0)
-            add_bias(j, 0)
-            add_bias(j, 1)
-            if s == 2:
-                add_bias(j, 2)
-                add_bias(j, 3)
-            gain_z(j + 1)
-            encode_mu(s)
-            if s > 2:
-                add_bias(j, 2)
-                add_bias(j, 3)
-                scale_x(s + 1, 2)
-            else:
-                quantize_x(s + 1)
-            quantize_z(j + 1)
-            row_max(j)
-            run(turn_x, s + 2, 2)
-            for c in range(CHUNKS):
-                decode(j + 1, c)
-            sum_squares(j, 0)
-            run(log_step, j - 1, 4)
-            copy_mu(s)
-            turn_z(s)
-            run(log_step, j - 1, 5)
-            run(widen, s + 3, 0)
-            run(log_step, j - 1, 6)
-            sum_squares(j, 1)
-            run(log_step, j - 1, 7)
+        encode_lv(2)
+        deviation(2)
+        sample(2)
+        for c in range(CHUNKS):
+            add_bias(0, c)
+        gain_z(1)
+        encode_mu(2)
+        quantize_x(3)
+        quantize_z(1)
+        row_max(0)
+        widen(4, 2)
+        copy_mu(2)
+        sum_lv(2)
+        turn_x(4, 0)
+        decode(1, 0)
+        decode(1, 1)
+        turn_z(2)
+        decode(1, 2)
+        decode(1, 3)
+        turn_x(4, 2)
+        widen(5, 0)
+        for term in range(2):
+            sum_squares(0, term)
 
         for s in range(3, LAST):
             j = s - 2
-            aside = 2 <= j + 1 <= 4
             scale_x(s + 1, 0)
-            if not 2 <= j <= 4:
+            if j not in BIAS_ASIDE:
                 add_bias(j, 0)
             gain_z(j + 1)
             if s > 3:
                 quantize_x(s)
             quantize_z(j + 1)
+            if s + 2 in VECTOR_WIDENS:
+                widen(s + 2, 2, 2, nc.vector.tensor_copy)
             run(finish, j - 2)
             run(turn_x, s + 2, 0)
             encode_lv(s)
@@ -521,13 +485,13 @@ def tile_linearvaeitemlogsoftmax_w8_kernel(
             encode_mu(s)
             sum_exp(j - 1)
             log_step(j - 1, 0)
-            run(widen, s + 2, 2)
+            if s + 2 not in VECTOR_WIDENS:
+                run(widen, s + 2, 2)
             log_step(j - 1, 1)
             deviation(s)
             sample(s)
             log_step(j - 1, 2)
-            if aside:
-                copy_chunk(j + 1)
+            if j + 1 in BIAS_ASIDE:
                 add_bias_aside(j + 1)
             log_step(j - 1, 3)
             copy_mu(s)
@@ -560,9 +524,9 @@ def tile_linearvaeitemlogsoftmax_w8_kernel(
         row_max(LAST - 2)
         for c in range(CHUNKS):
             decode(LAST - 1, c)
-        for step in range(2):
-            log_step(LAST - 3, step)
-            sum_squares(LAST - 2, step)
+        for term in range(2):
+            log_step(LAST - 3, term)
+            sum_squares(LAST - 2, term)
         log_step(LAST - 3, 2)
         deviation(LAST)
         sample(LAST)
@@ -571,40 +535,42 @@ def tile_linearvaeitemlogsoftmax_w8_kernel(
         turn_z(LAST)
         log_step(LAST - 3, 4)
         sum_lv(LAST)
-        for step in range(5, 8):
+        for step in range(5, LOG_STEPS):
             log_step(LAST - 3, step)
+
         sum_exp(LAST - 2)
         for c in range(CHUNKS - 1):
             add_bias(LAST - 1, c)
         gain_z(LAST)
-        add_bias(LAST - 1, 3)
+        add_bias(LAST - 1, CHUNKS - 1)
         quantize_z(LAST)
         finish(LAST - 3)
         row_max(LAST - 1)
         for c in range(CHUNKS):
             decode(LAST, c)
-        for step in range(8):
+        for term in range(2):
+            log_step(LAST - 2, term)
+            sum_squares(LAST - 1, term)
+        for step in range(2, LOG_STEPS):
             log_step(LAST - 2, step)
-            if step < 2:
-                sum_squares(LAST - 1, step)
+
         sum_exp(LAST - 1)
         add_bias(LAST, 0)
         add_bias(LAST, 1)
         finish(LAST - 2)
-        chunk_max(LAST, 0)
-        add_bias(LAST, 2)
-        chunk_max(LAST, 1)
-        add_bias(LAST, 3)
-        chunk_max(LAST, 2)
-        chunk_max(LAST, 3)
-        join_max(LAST)
         for c in range(CHUNKS):
-            for step in ((0, 1), (2, 3, 4), (5, 6, 7), ())[c]:
+            chunk_max(c)
+            if c + 2 < CHUNKS:
+                add_bias(LAST, c + 2)
+        nc.vector.tensor_reduce(out=neg_max[:, LAST:], in_=chunk_neg_max[:], axis=AXIS.X, op=ALU.min)
+        for c, steps in enumerate((range(0, 2), range(2, 5), range(5, LOG_STEPS))):
+            for step in steps:
                 log_step(LAST - 1, step)
-            chunk_exp(LAST, c)
-        finish_on_vector(LAST - 1)
-        chunk_weights(LAST)
-        join_sums(LAST)
+            chunk_exp(c)
+        chunk_exp(CHUNKS - 1)
+        finish_on_vector(LAST - 1, log_sum(LAST - 1), HALF)
+        join_chunks()
         sum_squares_on_vector(LAST)
-        finish_last(LAST)
+        nc.scalar.activation(out=log_total[:], in_=exp_sum[:, LAST:], func=ACT.Ln)
+        finish_on_vector(LAST, log_total[:], BANK)
         finish_kl()

import math
from contextlib import ExitStack

import concourse.mybir as mybir
from concourse.masks import make_identity

N, I, Z = 1024, 2048, 512
FLOPS = 3 * 2 * N * I * Z

F32 = mybir.dt.float32
BF16 = mybir.dt.bfloat16
I32 = mybir.dt.int32
U32 = mybir.dt.uint32
U8 = mybir.dt.uint8
FP8 = mybir.dt.float8_e4m3fn
FP8X4 = mybir.dt.float8_e4m3fn_x4
ALU = mybir.AluOpType
ACT = mybir.ActivationFunctionType
AXIS = mybir.AxisListType

P = 128
PACK = 4
K_PASS = P * PACK
TILES = N // P
LAST = TILES - 1
PASSES = I // K_PASS
HALVES = (0, 2)
BANK = 512
CHUNKS = I // BANK
HALF = I // 2
LN2 = math.log(2.0)
LOG_STEPS = 8

PSUM_BUFS = {"x_bank": 2, "t_bank": 4, "mu_bank": 1}
WM_SLOT, WV_SLOT, WD_SLOT = 0, 1, 2
WIDE_BUFS = 8
GROUPED_BUFS = 3
MU_SD_BUFS = 4
NOISE_BUFS = 3
LOGITS_BUFS = 6
BIAS_ASIDE = range(2, 5)
VECTOR_WIDENS = range(5, 7)


def tile_linearvaeitemlogsoftmax_w8_kernel(
    tc, x_bytes, x_scale, wm_words, wm_scales, wv_words, wv_scales, eps, g, wd_words, wd_scales, bd, out_0, out_1
):
    nc = tc.nc
    x_rows = x_bytes.rearrange("(p i) k -> p i k", i=TILES)
    eps_rows = eps.rearrange("(p i) z -> p i z", i=TILES)
    logp_rows = out_0.rearrange("(p i) n -> p i n", i=TILES)

    with ExitStack() as ctx:
        keep = ctx.enter_context(tc.tile_pool(name="keep", bufs=1))
        work = ctx.enter_context(tc.tile_pool(name="work", bufs=2))
        psum = ctx.enter_context(tc.psum_pool(name="psum", bufs=1))
        ctx.enter_context(tc.manual_schedule())

        bd_row = keep.tile([P, I], BF16)
        nc.vector.memset(bd_row[:].bitcast(I32), 0)
        ones = keep.tile([P, P], BF16)
        nc.vector.memset(ones[:], 1.0)
        w_scales = keep.tile([P, 3, BANK], U8, align_bytes=64)
        nc.vector.memset(w_scales[:].rearrange("p w n -> p (w n)").bitcast(I32), 0)
        ident = keep.tile([P, P], F32)
        make_identity(nc, ident[:])
        consts = keep.tile([P, 3], F32)
        for col, value in enumerate((-1.5, -1.0, -2.0)):
            nc.gpsimd.memset(consts[:, col : col + 1], value)
        minus_3_halves, minus_one, minus_two = (consts[:, col : col + 1] for col in range(3))

        x_sb = [keep.tile([P, I], U8, name="x_codes_%d" % i) for i in range(TILES)]
        x_scale_sb = keep.tile([P, PASSES, PACK], F32)
        wm_sb = keep.tile([P, PASSES, Z], U32, align_bytes=64)
        wv_sb = keep.tile([P, PASSES, Z], U32, align_bytes=64)
        wd_sb = keep.tile([P, I], U32, align_bytes=64)
        eps_sb = [keep.tile([P, 2, Z], BF16, name="eps_%d" % pair) for pair in range(TILES // 2)]
        g_sb = keep.tile([P, PACK], BF16)
        bd_sb = keep.tile([P, I], BF16)

        def load_x(i):
            nc.sync.dma_start(out=x_sb[i][:], in_=x_rows[:, i, :])

        def load_scales(slot, rows):
            for quad in range(4):
                nc.sync.dma_start(
                    out=w_scales[32 * quad : 32 * quad + 16, slot, :].bitcast(I32),
                    in_=rows[:, 4 * quad : 4 * quad + 4, :].bitcast(I32),
                )

        def load_words(dst, words):
            nc.sync.dma_start(out=dst[:].bitcast(I32), in_=words.rearrange("c p n t -> p c (n t)").bitcast(I32))

        def load_eps(i):
            nc.sync.dma_start(out=eps_sb[i // 2][:], in_=eps_rows[:, i : i + 2, :])

        load_x(0)
        nc.sync.dma_start(out=x_scale_sb[:], in_=x_scale.rearrange("o (c p t) -> p (o c) t", p=P, t=PACK))
        nc.sync.dma_start(out=bd_row[0:1, :], in_=bd.rearrange("(o n) -> o n", o=1))
        load_x(1)
        load_words(wv_sb, wv_words)
        load_scales(WV_SLOT, wv_scales)
        load_x(2)
        load_words(wm_sb, wm_words)
        load_eps(0)
        load_scales(WM_SLOT, wm_scales)
        load_x(3)
        nc.sync.dma_start(out=wd_sb[:].bitcast(I32), in_=wd_words[0].rearrange("p n t -> p (n t)").bitcast(I32))
        nc.sync.dma_start(out=g_sb[:], in_=g.rearrange("(p t) -> p t", t=PACK))
        load_scales(WD_SLOT, wd_scales[0].rearrange("r (c n) -> c r n", n=BANK))
        for i in range(4, TILES):
            load_x(i)
            if i % 2 == 0:
                load_eps(i - 2)
        load_eps(TILES - 2)

        neg_max = keep.tile([P, TILES], F32)
        neg_lse = keep.tile([P, TILES], F32)
        exp_sum = keep.tile([P, TILES], F32)
        lv_sum = keep.tile([P, TILES], F32)
        sq_sum = keep.tile([P, 2, TILES], F32)
        log_state = keep.tile([P, LOG_STEPS, TILES], F32)
        chunk_neg_max = keep.tile([P, CHUNKS], F32)
        chunk_sum = keep.tile([P, 2, CHUNKS], F32)
        chunk_term = keep.tile([P, CHUNKS], F32)
        log_total = keep.tile([P, 1], F32)

        bias_bank, wide, x_bank, x_grouped, x_mx, lv_bank, mu_bank, mu_sd = {}, {}, {}, {}, {}, {}, {}, {}
        noise, z_bank, z_grouped, z_mx, t_bank, logits = {}, {}, {}, {}, {}, {}

        def psum_tile(shape, dtype, bank):
            return psum.tile(shape, dtype, name=bank, bufs=PSUM_BUFS[bank])

        def spread_bias(half, bank):
            bias_bank[half] = psum_tile([P, HALF], BF16, bank)
            for c in range(2):
                src = slice(half * HALF + c * BANK, half * HALF + (c + 1) * BANK)
                dst = bias_bank[half][:, c * BANK : (c + 1) * BANK]
                nc.tensor.matmul(out=dst, lhsT=ones[:], rhs=bd_row[:, src], start=True, stop=True)

        def keep_bias(half):
            nc.scalar.copy(out=bd_sb[:, half * HALF : (half + 1) * HALF], in_=bias_bank[half][:])

        def widen(i, first, count=2, copy=nc.scalar.copy):
            wide[i, first] = work.tile([P, count * K_PASS], BF16, name="wide", bufs=WIDE_BUFS)
            copy(out=wide[i, first][:], in_=x_sb[i][:, first * K_PASS : (first + count) * K_PASS].bitcast(FP8))

        def turn_x(i, first, count=2, bank="x_bank"):
            x_bank[i, first] = psum_tile([P, 2, count, P], F32, bank)
            words = wide[i, first][:].bitcast(F32)
            for c in range(count):
                for u in range(2):
                    every_second = words[:, 2 * P * c + u : 2 * P * (c + 1) : 2]
                    nc.tensor.transpose(x_bank[i, first][:, u, c, :], every_second, ident[:])

        def scale_x(i, first, count=2):
            if first == 0:
                x_grouped[i] = work.tile([P, PASSES, P, PACK], BF16, name="x_grouped", bufs=GROUPED_BUFS, align_bytes=64)
            passes = slice(first, first + count)
            scale = x_scale_sb[:, passes, :].rearrange("p c (u e) -> p c u e", u=2)
            nc.vector.tensor_tensor(
                out=x_grouped[i][:, passes].rearrange("p c n (u e) -> p c n u e", u=2),
                in0=x_bank[i, first][:].bitcast(BF16).rearrange("p u c (n e) -> p c n u e", e=2),
                in1=scale.unsqueeze(2).broadcast_to([P, count, P, 2, 2]),
                op=ALU.mult,
            )

        def mx_tiles(name, columns):
            codes = work.tile([P, columns], U32, name=name + "_codes", align_bytes=64)
            scales = work.tile([P, columns], U8, name=name + "_scales", align_bytes=64)
            return codes, scales

        def quantize_x(i, first=0, count=PASSES):
            if first == 0:
                x_mx[i] = mx_tiles("xq", PASSES * P)
            codes, scales = x_mx[i]
            cols = slice(first * P, (first + count) * P)
            nc.vector.quantize_mx(
                out=codes[:, cols].bitcast(FP8X4),
                scales=scales[:, cols],
                in_=x_grouped[i][:, first : first + count].rearrange("p c n t -> p (c n t)"),
            )

        def encode(i, bank, w_sb, slot, passes):
            codes, scales = x_mx[i]
            for c in passes:
                cols = slice(c * P, (c + 1) * P)
                nc.tensor.matmul_mx(
                    out=bank[:],
                    lhsT=codes[:, cols].bitcast(FP8X4),
                    lhsT_scale=scales[:, cols],
                    rhs=w_sb[:, c, :].bitcast(FP8X4),
                    rhs_scale=w_scales[4 * c :, slot, :],
                    start=(c == 0),
                    stop=(c == PASSES - 1),
                )

        def encode_lv(i, first=0, count=PASSES):
            if first == 0:
                lv_bank[i] = psum.tile([P, Z], F32, name="lv_bank")
            encode(i, lv_bank[i], wv_sb, WV_SLOT, range(first, first + count))

        def encode_mu(i, first=0, count=PASSES):
            if first == 0:
                mu_bank[i] = psum_tile([P, Z], F32, "mu_bank")
            encode(i, mu_bank[i], wm_sb, WM_SLOT, range(first, first + count))

        def by_byte(ap):
            return ap.rearrange("p (m t) -> p t m", t=PACK)

        def unread(width):
            scratch = work.tile([P, I], BF16, name="unread")
            return scratch[:, :width]

        def deviation(i):
            mu_sd[i] = work.tile([P, 2, PACK, P], F32, name="mu_sd", bufs=MU_SD_BUFS)
            nc.scalar.activation(out=mu_sd[i][:, 1], in_=by_byte(lv_bank[i][:]), func=ACT.Exp, scale=0.5)

        def sum_lv(i):
            nc.scalar.activation(out=unread(Z), in_=lv_bank[i][:], func=ACT.Identity, accum_out=lv_sum[:, i : i + 1])

        def copy_mu(i):
            nc.scalar.copy(out=mu_sd[i][:, 0], in_=by_byte(mu_bank[i][:]))

        def sum_squares(i, term):
            nc.scalar.activation(
                out=unread(Z),
                in_=mu_sd[i][:, term].rearrange("p t m -> p (t m)"),
                func=ACT.Square,
                accum_out=sq_sum[:, term, i : i + 1],
            )

        def sum_squares_on_vector(i):
            for term in range(2):
                values = mu_sd[i][:, term].rearrange("p t m -> p (t m)")
                scratch = work.tile([P, Z], BF16, name="unread_of_vector")
                nc.vector.scalar_tensor_tensor(
                    out=scratch[:],
                    in0=values,
                    scalar=1.0,
                    in1=values,
                    op0=ALU.mult,
                    op1=ALU.mult,
                    accum_out=sq_sum[:, term, i : i + 1],
                )

        def sample(i):
            noise[i] = work.tile([P, PACK, P], F32, name="noise", bufs=NOISE_BUFS)
            nc.gpsimd.tensor_tensor(
                out=noise[i][:], in0=mu_sd[i][:, 1], in1=by_byte(eps_sb[i // 2][:, i % 2, :]), op=ALU.mult
            )

        def turn_z(i):
            z_bank[i] = psum_tile([P, PACK, P], F32, "mu_bank")
            for t in range(PACK):
                for opens, term in ((True, mu_sd[i][:, 0, t, :]), (False, noise[i][:, t, :])):
                    nc.tensor.matmul(
                        out=z_bank[i][:, t, :], lhsT=term, rhs=ident[:], is_transpose=True, start=opens, stop=not opens
                    )

        def gain_z(i):
            z_grouped[i] = work.tile([P, P, PACK], BF16, name="z_grouped", align_bytes=64)
            nc.vector.tensor_tensor(
                out=z_grouped[i][:],
                in0=z_bank[i][:].rearrange("p t n -> p n t"),
                in1=g_sb[:].unsqueeze(1).broadcast_to([P, P, PACK]),
                op=ALU.mult,
            )

        def quantize_z(i):
            z_mx[i] = mx_tiles("zq", P)
            codes, scales = z_mx[i]
            nc.vector.quantize_mx(
                out=codes[:].bitcast(FP8X4), scales=scales[:], in_=z_grouped[i][:].rearrange("p n t -> p (n t)")
            )

        def decode(i, c):
            t_bank[i, c] = psum_tile([P, BANK], F32, "t_bank")
            codes, scales = z_mx[i]
            nc.tensor.matmul_mx(
                out=t_bank[i, c][:],
                lhsT=codes[:].bitcast(FP8X4),
                lhsT_scale=scales[:],
                rhs=wd_sb[:, c * BANK : (c + 1) * BANK].bitcast(FP8X4),
                rhs_scale=w_scales[4 * c :, WD_SLOT, :],
                start=True,
                stop=True,
            )

        def new_logits(i):
            logits[i] = work.tile([P, I], F32, name="logits", bufs=LOGITS_BUFS)

        def add_bias(i, c):
            if c == 0:
                new_logits(i)
            cols = slice(c * BANK, (c + 1) * BANK)
            nc.vector.tensor_tensor(out=logits[i][:, cols], in0=t_bank[i, c][:], in1=bd_sb[:, cols], op=ALU.add)

        def add_bias_aside(i):
            new_logits(i)
            chunk = logits[i][:, :BANK]
            nc.scalar.copy(out=chunk, in_=t_bank[i, 0][:])
            nc.gpsimd.tensor_tensor(out=chunk, in0=chunk, in1=bd_sb[:, :BANK], op=ALU.add)

        def row_max(i):
            nc.vector.tensor_reduce(out=neg_max[:, i : i + 1], in_=logits[i][:], axis=AXIS.X, op=ALU.max, negate=True)

        def sum_exp(i):
            nc.scalar.activation(
                out=unread(I),
                in_=logits[i][:],
                func=ACT.Exp,
                bias=neg_max[:, i : i + 1],
                accum_out=exp_sum[:, i : i + 1],
            )

        def log_step(i, step):
            total = exp_sum[:, i : i + 1]
            u0, e0, square, u1, e1, u2, e2, u3 = (log_state[:, row, i : i + 1] for row in range(LOG_STEPS))
            out, in_, func, scale, bias = (
                (u0, total.bitcast(U32), ACT.Copy, LN2 / 2**23, (0.043 - 127.0) * LN2 - 1.5),
                (e0, u0, ACT.Exp, -1.0, minus_3_halves),
                (square, e0, ACT.Square, total, minus_two),
                (u1, square, ACT.Identity, -0.5, u0),
                (e1, u1, ACT.Exp, -1.0, minus_two),
                (u2, e1, ACT.Identity, total, u1),
                (e2, u2, ACT.Exp, -1.0, minus_one),
                (u3, e2, ACT.Identity, total, u2),
            )[step]
            nc.scalar.activation(out=out, in_=in_, func=func, scale=scale, bias=bias)

        def log_sum(i):
            return log_state[:, LOG_STEPS - 1, i : i + 1]

        def finish(i):
            col = slice(i, i + 1)
            nc.vector.tensor_tensor(out=neg_lse[:, col], in0=neg_max[:, col], in1=log_sum(i), op=ALU.subtract)
            nc.gpsimd.tensor_scalar(
                out=logits[i][:], in0=logits[i][:], scalar1=1.0, scalar2=neg_lse[:, col], op0=ALU.mult, op1=ALU.add
            )
            nc.sync.dma_start(out=logp_rows[:, i, :], in_=logits[i][:])

        def finish_on_vector(i, log_of_sum, width):
            for start in range(0, I, width):
                cols = slice(start, start + width)
                nc.vector.tensor_scalar(
                    out=logits[i][:, cols],
                    in0=logits[i][:, cols],
                    scalar1=neg_max[:, i : i + 1],
                    scalar2=log_of_sum,
                    op0=ALU.add,
                    op1=ALU.subtract,
                )
                nc.sync.dma_start(out=logp_rows[:, i, cols], in_=logits[i][:, cols])

        def chunk_max(c):
            cols = slice(c * BANK, (c + 1) * BANK)
            nc.vector.tensor_reduce(
                out=chunk_neg_max[:, c : c + 1], in_=logits[LAST][:, cols], axis=AXIS.X, op=ALU.max, negate=True
            )

        def chunk_exp(c):
            nc.scalar.activation(
                out=unread(BANK),
                in_=logits[LAST][:, c * BANK : (c + 1) * BANK],
                func=ACT.Exp,
                bias=chunk_neg_max[:, c : c + 1],
                accum_out=chunk_sum[:, 0, c : c + 1],
            )

        def join_chunks():
            nc.scalar.activation(
                out=chunk_sum[:, 1], in_=chunk_neg_max[:], func=ACT.Exp, scale=-1.0, bias=neg_max[:, LAST:]
            )
            nc.vector.scalar_tensor_tensor(
                out=chunk_term[:],
                in0=chunk_sum[:, 0],
                scalar=1.0,
                in1=chunk_sum[:, 1],
                op0=ALU.mult,
                op1=ALU.mult,
                accum_out=exp_sum[:, LAST:],
            )

        def finish_kl():
            kl = keep.tile([P, TILES], F32)
            nc.vector.tensor_tensor(out=kl[:], in0=sq_sum[:, 1], in1=lv_sum[:], op=ALU.subtract)
            nc.vector.tensor_tensor(out=kl[:], in0=kl[:], in1=sq_sum[:, 0], op=ALU.add)
            nc.vector.tensor_scalar(out=kl[:], in0=kl[:], scalar1=0.5 / Z, scalar2=-0.5, op0=ALU.mult, op1=ALU.add)
            nc.sync.dma_start(out=out_1.rearrange("(p i) -> p i", i=TILES), in_=kl[:])

        def run(stage, i, *args):
            if 0 <= i < TILES:
                stage(i, *args)

        spread_bias(0, "mu_bank")
        for c in range(PASSES):
            widen(0, c, 1, nc.vector.tensor_copy)
            turn_x(0, c, 1, "t_bank")
        for first in HALVES:
            widen(1, first)
        for c in range(PASSES - 1):
            scale_x(0, c, 1)
        quantize_x(0, 0, 2)
        scale_x(0, PASSES - 1, 1)
        quantize_x(0, 2, 2)
        spread_bias(1, "t_bank")
        for half in range(2):
            keep_bias(half)
        for first in HALVES:
            widen(2, first)
            turn_x(1, first)
            encode_lv(0, first, 2)
            scale_x(1, first)
        deviation(0)
        sample(0)
        sum_lv(0)
        for first in HALVES:
            widen(3, first)
            turn_x(2, first)
            encode_mu(0, first, 2)
        copy_mu(0)
        scale_x(2, 0)
        quantize_x(1)
        scale_x(2, 2)
        turn_x(3, 0)
        encode_lv(1, 0, 2)
        turn_z(0)
        turn_x(3, 2)
        encode_lv(1, 2, 2)
        scale_x(3, 0)
        gain_z(0)
        quantize_x(2)
        quantize_z(0)
        scale_x(3, 2)
        encode_mu(1)
        for c in range(CHUNKS):
            decode(0, c)
        deviation(1)
        sample(1)
        sum_lv(1)
        copy_mu(1)
        widen(4, 0)
        turn_z(1)

        encode_lv(2)
        deviation(2)
        sample(2)
        for c in range(CHUNKS):
            add_bias(0, c)
        gain_z(1)
        encode_mu(2)
        quantize_x(3)
        quantize_z(1)
        row_max(0)
        widen(4, 2)
        copy_mu(2)
        sum_lv(2)
        turn_x(4, 0)
        decode(1, 0)
        decode(1, 1)
        turn_z(2)
        decode(1, 2)
        decode(1, 3)
        turn_x(4, 2)
        widen(5, 0)
        for term in range(2):
            sum_squares(0, term)

        for s in range(3, LAST):
            j = s - 2
            scale_x(s + 1, 0)
            if j not in BIAS_ASIDE:
                add_bias(j, 0)
            gain_z(j + 1)
            if s > 3:
                quantize_x(s)
            quantize_z(j + 1)
            if s + 2 in VECTOR_WIDENS:
                widen(s + 2, 2, 2, nc.vector.tensor_copy)
            run(finish, j - 2)
            run(turn_x, s + 2, 0)
            encode_lv(s)
            decode(j + 1, 0)
            encode_mu(s)
            sum_exp(j - 1)
            log_step(j - 1, 0)
            if s + 2 not in VECTOR_WIDENS:
                run(widen, s + 2, 2)
            log_step(j - 1, 1)
            deviation(s)
            sample(s)
            log_step(j - 1, 2)
            if j + 1 in BIAS_ASIDE:
                add_bias_aside(j + 1)
            log_step(j - 1, 3)
            copy_mu(s)
            log_step(j - 1, 4)
            sum_lv(s)
            log_step(j - 1, 5)
            sum_squares(j, 0)
            log_step(j - 1, 6)
            for c in range(1, CHUNKS):
                add_bias(j, c)
            scale_x(s + 1, 2)
            row_max(j)
            run(turn_x, s + 2, 2)
            turn_z(s)
            for c in range(1, CHUNKS):
                decode(j + 1, c)
            run(widen, s + 3, 0)
            log_step(j - 1, 7)
            sum_squares(j, 1)

        quantize_x(LAST)
        finish(LAST - 4)
        encode_lv(LAST)
        sum_exp(LAST - 3)
        gain_z(LAST - 1)
        encode_mu(LAST)
        for c in range(CHUNKS):
            add_bias(LAST - 2, c)
        quantize_z(LAST - 1)
        row_max(LAST - 2)
        for c in range(CHUNKS):
            decode(LAST - 1, c)
        for term in range(2):
            log_step(LAST - 3, term)
            sum_squares(LAST - 2, term)
        log_step(LAST - 3, 2)
        deviation(LAST)
        sample(LAST)
        log_step(LAST - 3, 3)
        copy_mu(LAST)
        turn_z(LAST)
        log_step(LAST - 3, 4)
        sum_lv(LAST)
        for step in range(5, LOG_STEPS):
            log_step(LAST - 3, step)

        sum_exp(LAST - 2)
        for c in range(CHUNKS - 1):
            add_bias(LAST - 1, c)
        gain_z(LAST)
        add_bias(LAST - 1, CHUNKS - 1)
        quantize_z(LAST)
        finish(LAST - 3)
        row_max(LAST - 1)
        for c in range(CHUNKS):
            decode(LAST, c)
        for term in range(2):
            log_step(LAST - 2, term)
            sum_squares(LAST - 1, term)
        for step in range(2, LOG_STEPS):
            log_step(LAST - 2, step)

        sum_exp(LAST - 1)
        add_bias(LAST, 0)
        add_bias(LAST, 1)
        finish(LAST - 2)
        for c in range(CHUNKS):
            chunk_max(c)
            if c + 2 < CHUNKS:
                add_bias(LAST, c + 2)
        nc.vector.tensor_reduce(out=neg_max[:, LAST:], in_=chunk_neg_max[:], axis=AXIS.X, op=ALU.min)
        for c, steps in enumerate((range(0, 2), range(2, 5), range(5, LOG_STEPS))):
            for step in steps:
                log_step(LAST - 1, step)
            chunk_exp(c)
        chunk_exp(CHUNKS - 1)
        finish_on_vector(LAST - 1, log_sum(LAST - 1), HALF)
        join_chunks()
        sum_squares_on_vector(LAST)
        nc.scalar.activation(out=log_total[:], in_=exp_sum[:, LAST:], func=ACT.Ln)
        finish_on_vector(LAST, log_total[:], BANK)
        finish_kl()
